import numpy as np
import ml_dtypes


def mxq(x, axis, fmt="e4m3"):
    dtype, down = {"e4m3": (ml_dtypes.float8_e4m3fn, 7), "e5m2": (ml_dtypes.float8_e5m2, 14)}[fmt]
    v = np.moveaxis(np.asarray(x, np.float32).astype(ml_dtypes.bfloat16).astype(np.float64), axis, -1)
    blocks = v.reshape(v.shape[:-1] + (-1, 32))
    amax = np.abs(blocks).max(-1, keepdims=True)
    byte = np.maximum(np.where(amax > 0, np.frexp(amax)[1] - 1 + 127, 0) - down, 1)
    scale = np.exp2(byte - 127.0)
    codes = (blocks / scale).astype(np.float32).astype(dtype).astype(np.float64)
    return np.moveaxis((codes * scale).reshape(v.shape), -1, axis)


WIDE = False


def mx_kscale(k):
    if not WIDE:
        return np.ones(k)
    levels = np.array([10, -10, 5, -5, 0])
    if k % 512:
        return np.exp2(np.random.permutation(np.resize(levels, k // 32))).repeat(32)
    a = np.empty((k // 512, 16))
    for p in range(k // 512):
        a[p, :8] = np.random.permutation(np.resize(levels, 8))
        for g in range(8):
            far = levels[np.abs(levels - a[p, g]) >= 10]
            a[p, g + 8] = far[np.random.randint(len(far))]
    return np.exp2(a.ravel()).repeat(32)


def f64(x):
    return np.asarray(x).astype(np.float64)


def striped(idx):
    return np.tile(idx.reshape(-1, 16).T, (8, 1)).astype(np.uint16)


def unstriped(offs):
    return offs[:16].T.reshape(-1).astype(np.int64)


E2M1 = np.array([0.0, 0.5, 1.0, 1.5, 2.0, 3.0, 4.0, 6.0, -0.0, -0.5, -1.0, -1.5, -2.0, -3.0, -4.0, -6.0])


def pack_weight(w, fmt):
    k, n = w.shape
    w = f64(np.asarray(w, np.float32).astype(ml_dtypes.bfloat16)).reshape(k // 32, 32, n)
    amax = np.abs(w).max(1)
    if fmt == "e4m3":
        byte = np.frexp(amax)[1] - 1 + 127 - 7
    else:
        mant, ex = np.frexp(amax / 6.0)
        byte = np.where(mant > 0.5, ex, ex - 1) + 127
    byte = np.clip(np.where(amax > 0, byte, 1), 1, 254)
    scaled = (w * np.exp2(127.0 - byte)[:, None, :]).reshape(k, n).astype(np.float32)
    by_word = np.ascontiguousarray(scaled.reshape(k // 512, 128, 4, n).transpose(0, 1, 3, 2))
    if fmt == "e4m3":
        words = by_word.astype(ml_dtypes.float8_e4m3fn).view(np.uint8)
    else:
        c = by_word.astype(ml_dtypes.float4_e2m1fn).view(np.uint8) & 0xF
        words = (c[..., 0::2] | (c[..., 1::2] << 4)).reshape(k // 512, 128, 2 * n)
    return np.ascontiguousarray(words), np.ascontiguousarray(byte.astype(np.uint8).reshape(k // 512, 16, n))


def unpack_weight(words, scales, fmt):
    g, _, n = scales.shape
    words = np.ascontiguousarray(words).reshape(g, 128, n, -1)
    if fmt == "e4m3":
        vals = words.view(ml_dtypes.float8_e4m3fn).astype(np.float64)
    else:
        nib = np.empty((g, 128, n, 4), np.uint8)
        nib[..., 0::2] = words & 0xF
        nib[..., 1::2] = words >> 4
        vals = E2M1[nib]
    vals = vals * np.repeat(np.exp2(scales.astype(np.float64) - 127.0), 8, axis=1)[..., None]
    return vals.transpose(0, 1, 3, 2).reshape(g * 512, n)


def silu(v):
    return v / (1.0 + np.exp(-np.maximum(v, -700.0)))


K, T, E, C, H, N = 512, 1024, 6, 128, 512, 128


def by_expert(wq, xq):
    return np.concatenate([wq[e].T @ xq[:, e * C:(e + 1) * C] for e in range(E)], axis=1)


def setup_inputs():
    n = np.random.standard_normal
    s = mx_kscale(K)[:, None]
    u = mx_kscale(H)
    w1 = [pack_weight(m, "e2m1") for m in n((E + 1, K, H)) / np.sqrt(K) / s[None]]
    w3 = [pack_weight(m, "e2m1") for m in n((E + 1, K, H)) / np.sqrt(K) / s[None] * u[None, None, :]]
    w2 = [pack_weight(m, "e2m1") for m in n((E + 1, H, N)) / np.sqrt(H) / u[None, :, None]]
    return {
        "xT": (n((K, T)) * s).astype(np.float32),
        "w1_words": np.stack([m[0] for m in w1]),
        "w1_scales": np.stack([m[1] for m in w1]),
        "w3_words": np.stack([m[0] for m in w3]),
        "w3_scales": np.stack([m[1] for m in w3]),
        "w2_words": np.stack([m[0] for m in w2]),
        "w2_scales": np.stack([m[1] for m in w2]),
        "gate": np.tile(np.random.uniform(0.2, 1.0, E * C), (N, 1)).astype(np.float32),
        "offs": striped(np.random.permutation(T)[:E * C]),
    }


def reference(xT, w1_words, w1_scales, w3_words, w3_scales, w2_words, w2_scales, gate, offs):
    idx = unstriped(offs)
    w1 = np.stack([unpack_weight(w1_words[e], w1_scales[e], "e2m1") for e in range(E + 1)])
    w3 = np.stack([unpack_weight(w3_words[e], w3_scales[e], "e2m1") for e in range(E + 1)])
    w2 = np.stack([unpack_weight(w2_words[e], w2_scales[e], "e2m1") for e in range(E + 1)])
    w1q, w3q, w2q = w1, w3, w2
    xs = mxq(f64(xT), 0, "e4m3")
    hs = silu(w1q[E].T @ xs) * (w3q[E].T @ xs)
    ys = w2q[E].T @ mxq(hs, 0, "e4m3")
    xq = mxq(f64(xT)[:, idx], 0, "e4m3")
    h = silu(by_expert(w1q, xq))
    h = h * by_expert(w3q, xq)
    y = by_expert(w2q, mxq(h, 0, "e4m3"))
    out = ys
    out[:, idx] += f64(gate) * y
    return out

@@ -1,0 +1,211 @@
+from contextlib import ExitStack
+
+import concourse.mybir as mybir
+from concourse.masks import make_identity
+
+F32 = mybir.dt.float32
+BF16 = mybir.dt.bfloat16
+I32 = mybir.dt.int32
+U32 = mybir.dt.uint32
+U16 = mybir.dt.uint16
+U8 = mybir.dt.uint8
+FP8X4 = mybir.dt.float8_e4m3fn_x4
+FP4X4 = mybir.dt.float4_e2m1fn_x4
+SILU = mybir.ActivationFunctionType.Silu
+MULT = mybir.AluOpType.mult
+ADD = mybir.AluOpType.add
+
+P = 128
+K, T, E, C, H, N = 512, 1024, 6, 128, 512, 128
+SHARED = E
+UNIT = 256
+TILES = UNIT // P
+FLOPS = 2 * (E * C + T) * (2 * K * H + H * N)
+
+
+def tile_moe_shr_glu_silu_kernel(tc, xT, w1_words, w1_scales, w3_words, w3_scales, w2_words, w2_scales, gate, offs, out):
+    nc = tc.nc
+    with ExitStack() as ctx:
+        keep = ctx.enter_context(tc.tile_pool(name="keep", bufs=1))
+        work = ctx.enter_context(tc.tile_pool(name="work", bufs=3))
+        psum = ctx.enter_context(tc.psum_pool(name="psum", bufs=2))
+
+        offsets = keep.tile([P, E * C // 16], U16, name="offsets")
+        raw = [keep.tile([P, 4, UNIT], F32, name=f"raw{c}") for c in range(4)]
+        pairs = keep.tile([P, 2, 2 * T], BF16, name="pairs", align_bytes=64)
+        w1 = keep.tile([P, E + 1, 2 * H], U8, name="w1", align_bytes=64)
+        w3 = keep.tile([P, E + 1, 2 * H], U8, name="w3", align_bytes=64)
+        w2 = keep.tile([P, E + 1, 2 * N], U8, name="w2", align_bytes=64)
+        s1 = keep.tile([P, E + 1, H], U8, name="s1", align_bytes=64)
+        s3 = keep.tile([P, E + 1, H], U8, name="s3", align_bytes=64)
+        s2 = keep.tile([P, E + 1, N], U8, name="s2", align_bytes=64)
+        gates = keep.tile([P, E * C], F32, name="gates")
+        scattered = keep.tile([P, T], F32, name="scattered")
+        result = keep.tile([P, T], F32, name="result")
+        early = keep.tile([P, 2 * UNIT], F32, name="early")
+        ident = keep.tile([P, P], F32, name="ident")
+        warm = keep.tile([P, 1], F32, name="warm")
+
+        def zero(eng, t):
+            eng.memset(t[:].rearrange("p e n -> p (e n)").bitcast(I32), 0)
+
+        nc.vector.memset(warm[:], 0.0)
+        nc.scalar.activation(warm[:], warm[:], SILU)
+        zero(nc.vector, s1)
+        zero(nc.vector, s3)
+        zero(nc.vector, s2)
+        make_identity(nc, ident[:])
+
+        def load_x(c):
+            nc.sync.dma_start(out=raw[c][:], in_=xT.rearrange("(p j) t -> p j t", j=4)[:, :, c * UNIT : (c + 1) * UNIT])
+
+        def load_words(tile, words, a, b):
+            nc.sync.dma_start(
+                out=tile[:, a:b, :].bitcast(I32),
+                in_=words[a:b, 0].bitcast(I32).rearrange("e p n -> p e n"),
+            )
+
+        def load_scales(eng, tile, scales):
+            view = scales.bitcast(I32).rearrange("e s (q r) n -> r q (e s) n", r=4)
+            for r in range(4):
+                eng.dma_start(out=tile[r:P:32, :, :].bitcast(I32), in_=view[r])
+
+        load_x(0)
+        load_words(w1, w1_words, SHARED, SHARED + 1)
+        load_words(w3, w3_words, SHARED, SHARED + 1)
+        load_scales(nc.scalar, s1, w1_scales)
+        load_scales(nc.gpsimd, s3, w3_scales)
+        load_x(1)
+        load_x(2)
+        nc.sync.dma_start(offsets[:], offs)
+        load_x(3)
+        load_words(w2, w2_words, 0, E + 1)
+        load_scales(nc.gpsimd, s2, w2_scales)
+        for a in (0, 2, 4):
+            load_words(w1, w1_words, a, a + 2)
+            load_words(w3, w3_words, a, a + 2)
+            if a == 0:
+                nc.sync.dma_start(out=gates[:], in_=gate)
+
+        nc.gpsimd.memset(scattered[:], 0.0)
+
+        def interleave(c, copy):
+            quads = work.tile([P, UNIT, 4], BF16, name="quads", align_bytes=64)
+            copy(quads[:].rearrange("p (c i) j -> p c j i", i=4), raw[c][:].rearrange("p j (c i) -> p c j i", i=4))
+            return quads[:].rearrange("p c j -> p (c j)")
+
+        def make_pairs(c, copy):
+            copy(
+                pairs[:, :, c * 2 * UNIT : (c + 1) * 2 * UNIT].rearrange("p h (t e) -> p h t e", e=2),
+                raw[c][:].rearrange("p (h e) t -> p h t e", e=2),
+            )
+
+        def gather(u):
+            quads = work.tile([P, UNIT, 4], BF16, name="quads", align_bytes=64)
+            flat = quads[:].rearrange("p c j -> p (c j)")
+            words = flat.bitcast(U32).rearrange("p (c h) -> p c h", h=2)
+            for h in range(2):
+                nc.vector.tensor_copy(
+                    words[:, :, h],
+                    pairs[:, h, :].bitcast(U32).indirect(offsets[:, u * UNIT // 16 : (u + 1) * UNIT // 16]),
+                )
+            return flat
+
+        def quantize(tag, flat):
+            width = flat.shape[1] // 4
+            codes = work.tile([P, width], U32, name=tag + "_codes", align_bytes=64)
+            scales = work.tile([P, width], U8, name=tag + "_scales", align_bytes=64)
+            nc.vector.quantize_mx(out=codes[:].bitcast(FP8X4), scales=scales[:], in_=flat)
+            return codes, scales
+
+        def finish(y, at):
+            cols = slice(at, at + y.shape[1])
+            nc.vector.tensor_tensor(result[:, cols], y[:], scattered[:, cols], ADD)
+            nc.sync.dma_start(out=out[:, cols], in_=result[:, cols])
+
+        def hidden(codes, scales, experts):
+            tiles = len(experts)
+            back = psum.tile([P, tiles, 2, P], F32, name="back")
+            for t, e in enumerate(experts):
+                cols = slice(t * P, (t + 1) * P)
+                a = psum.tile([P, H], F32, name="a")
+                b = psum.tile([P, H], F32, name="b")
+                for acc, w, s in ((a, w1, s1), (b, w3, s3)):
+                    nc.tensor.matmul_mx(
+                        out=acc[:], lhsT=codes[:, cols].bitcast(FP8X4), lhsT_scale=scales[:, cols],
+                        rhs=w[:, e, :].bitcast(FP4X4), rhs_scale=s[:, e, :], start=True, stop=True,
+                    )
+                act = work.tile([P, H], F32, name="act")
+                nc.scalar.activation(
+                    act[:].rearrange("p (u m e) -> p u m e", u=2, e=2),
+                    a[:].rearrange("p (m u e) -> p u m e", u=2, e=2),
+                    SILU,
+                )
+                h = work.tile([P, H], BF16, name="h")
+                nc.vector.tensor_tensor(
+                    h[:].rearrange("p (u m e) -> p u m e", u=2, e=2),
+                    act[:].rearrange("p (u m e) -> p u m e", u=2, e=2),
+                    b[:].rearrange("p (m u e) -> p u m e", u=2, e=2),
+                    MULT,
+                )
+                hw = h[:].bitcast(F32)
+                for u in range(2):
+                    nc.tensor.transpose(back[:, t, u, :], hw[:, u * P : (u + 1) * P], ident[:])
+            turned = work.tile([P, tiles * P, 4], BF16, name="turned", align_bytes=64)
+            flat = turned[:].rearrange("p c j -> p (c j)")
+            nc.scalar.copy(
+                flat.bitcast(F32).rearrange("p (t r u) -> p t r u", t=tiles, u=2),
+                back[:].rearrange("p t u r -> p t r u"),
+            )
+            return quantize("h", flat)
+
+        def last(y, codes, scales, experts):
+            for t, e in enumerate(experts):
+                cols = slice(t * P, (t + 1) * P)
+                nc.tensor.matmul_mx(
+                    out=y[:, cols], lhsT=w2[:, e, :].bitcast(FP4X4), lhsT_scale=s2[:, e, :],
+                    rhs=codes[:, cols].bitcast(FP8X4), rhs_scale=scales[:, cols], start=True, stop=True,
+                )
+
+        def shared_unit(c, copy):
+            flat = interleave(c, copy)
+            codes, scales = quantize("x", flat)
+            hc, hs = hidden(codes, scales, (SHARED,) * TILES)
+            y = psum.tile([P, UNIT], F32, name="y")
+            last(y, hc, hs, (SHARED,) * TILES)
+            return y
+
+        def routed_unit(u):
+            flat = gather(u)
+            codes, scales = quantize("x", flat)
+            experts = tuple(range(u * TILES, (u + 1) * TILES))
+            hc, hs = hidden(codes, scales, experts)
+            y = psum.tile([P, UNIT], F32, name="y")
+            last(y, hc, hs, experts)
+            ysb = work.tile([P, UNIT], F32, name="ysb")
+            nc.scalar.copy(ysb[:], y[:])
+            nc.vector.tensor_tensor(
+                scattered[:].indirect(offsets[:, u * UNIT // 16 : (u + 1) * UNIT // 16]),
+                ysb[:], gates[:, u * UNIT : (u + 1) * UNIT], MULT,
+            )
+
+        y = shared_unit(0, nc.vector.tensor_copy)
+        nc.scalar.copy(early[:, 0:UNIT], y[:])
+        y = shared_unit(1, nc.scalar.copy)
+        nc.scalar.copy(early[:, UNIT : 2 * UNIT], y[:])
+        for c in range(4):
+            make_pairs(c, nc.vector.tensor_copy)
+        for u in range(3):
+            routed_unit(u)
+        half = slice(0, 2 * UNIT)
+        nc.vector.tensor_tensor(result[:, half], early[:], scattered[:, half], ADD)
+        nc.sync.dma_start(out=out[:, half], in_=result[:, half])
+        y = shared_unit(2, nc.scalar.copy)
+        finish(y, 2 * UNIT)
+        codes, scales = quantize("x", interleave(3, nc.scalar.copy))
+        for t in range(TILES):
+            cols = slice(t * P, (t + 1) * P)
+            hc, hs = hidden(codes[:, cols], scales[:, cols], (SHARED,))
+            y = psum.tile([P, P], F32, name="y")
+            last(y, hc, hs, (SHARED,))
+            finish(y, 3 * UNIT + t * P)

@@ -27,89 +27,106 @@ def tile_moe_shr_glu_silu_kernel(tc, xT, w1_words, w1_scales, w3_words, w3_scale
     nc = tc.nc
     with ExitStack() as ctx:
         keep = ctx.enter_context(tc.tile_pool(name="keep", bufs=1))
-        work = ctx.enter_context(tc.tile_pool(name="work", bufs=3))
-        psum = ctx.enter_context(tc.psum_pool(name="psum", bufs=2))
+        reuse = ctx.enter_context(tc.tile_pool(name="reuse", bufs=1))
+        work = ctx.enter_context(tc.tile_pool(name="work", bufs=7))
+        psum = ctx.enter_context(tc.psum_pool(name="psum", bufs=1))
 
         offsets = keep.tile([P, E * C // 16], U16, name="offsets")
-        raw = [keep.tile([P, 4, UNIT], F32, name=f"raw{c}") for c in range(4)]
-        pairs = keep.tile([P, 2, 2 * T], BF16, name="pairs", align_bytes=64)
-        w1 = keep.tile([P, E + 1, 2 * H], U8, name="w1", align_bytes=64)
-        w3 = keep.tile([P, E + 1, 2 * H], U8, name="w3", align_bytes=64)
-        w2 = keep.tile([P, E + 1, 2 * N], U8, name="w2", align_bytes=64)
-        s1 = keep.tile([P, E + 1, H], U8, name="s1", align_bytes=64)
-        s3 = keep.tile([P, E + 1, H], U8, name="s3", align_bytes=64)
-        s2 = keep.tile([P, E + 1, N], U8, name="s2", align_bytes=64)
-        gates = keep.tile([P, E * C], F32, name="gates")
+        pairs = keep.tile([P, 2, T], U32, name="pairs", align_bytes=64)
+        w1 = keep.tile([P, E, 2 * H], U8, name="w1", align_bytes=64)
+        w3 = keep.tile([P, E, 2 * H], U8, name="w3", align_bytes=64)
+        shared_w = [keep.tile([P, 2 * H], U8, name=f"shared_w{m}", align_bytes=64) for m in range(2)]
+        shared_s = [keep.tile([P, H], U8, name=f"shared_s{m}", align_bytes=64) for m in range(2)]
+        planes = keep.tile([P, 2, E, H], U8, name="planes", align_bytes=64)
+        s1 = planes[:, 0]
+        s3 = planes[:, 1]
+        hidden_codes = keep.tile([P, T], U32, name="hidden_codes", align_bytes=64)
+        hidden_scales = keep.tile([P, T], U8, name="hidden_scales", align_bytes=64)
         scattered = keep.tile([P, T], F32, name="scattered")
         result = keep.tile([P, T], F32, name="result")
-        early = keep.tile([P, 2 * UNIT], F32, name="early")
         ident = keep.tile([P, P], F32, name="ident")
-        warm = keep.tile([P, 1], F32, name="warm")
+
+        warm = reuse.tile([P, 16], F32, name="warm", offset=3 * 4096 - 32)
+
+        raw = [reuse.tile([P, 4, UNIT], F32, name=f"raw{c}", offset=c * 4096, align_bytes=64) for c in range(4)]
+        w2 = reuse.tile([P, E + 1, 2 * N], U8, name="w2", offset=4096, align_bytes=64)
+        s2 = reuse.tile([P, E + 1, N], U8, name="s2", offset=6144, align_bytes=64)
+        gates = reuse.tile([P, E * C], F32, name="gates", offset=8192, align_bytes=64)
 
         def zero(eng, t):
-            eng.memset(t[:].rearrange("p e n -> p (e n)").bitcast(I32), 0)
-
-        nc.vector.memset(warm[:], 0.0)
-        nc.scalar.activation(warm[:], warm[:], SILU)
-        zero(nc.vector, s1)
-        zero(nc.vector, s3)
-        zero(nc.vector, s2)
-        make_identity(nc, ident[:])
+            eng.memset(t.rearrange("p e n -> p (e n)").bitcast(I32), 0)
 
         def load_x(c):
             nc.sync.dma_start(out=raw[c][:], in_=xT.rearrange("(p j) t -> p j t", j=4)[:, :, c * UNIT : (c + 1) * UNIT])
 
         def load_words(tile, words, a, b):
-            nc.sync.dma_start(
-                out=tile[:, a:b, :].bitcast(I32),
-                in_=words[a:b, 0].bitcast(I32).rearrange("e p n -> p e n"),
-            )
+            nc.sync.dma_start(out=tile.bitcast(I32), in_=words[a:b, 0].bitcast(I32).rearrange("e p n -> p e n"))
 
-        def load_scales(eng, tile, scales):
-            view = scales.bitcast(I32).rearrange("e s (q r) n -> r q (e s) n", r=4)
+        def load_scales(eng, tile, scales, a, b):
+            view = scales[a:b].bitcast(I32).rearrange("e s (q r) n -> r q (e s) n", r=4)
             for r in range(4):
-                eng.dma_start(out=tile[r:P:32, :, :].bitcast(I32), in_=view[r])
+                eng.dma_start(out=tile[r:P:32, 0 : b - a, :].bitcast(I32), in_=view[r])
 
-        load_x(0)
-        load_words(w1, w1_words, SHARED, SHARED + 1)
-        load_words(w3, w3_words, SHARED, SHARED + 1)
-        load_scales(nc.scalar, s1, w1_scales)
-        load_scales(nc.gpsimd, s3, w3_scales)
-        load_x(1)
-        load_x(2)
-        nc.sync.dma_start(offsets[:], offs)
-        load_x(3)
-        load_words(w2, w2_words, 0, E + 1)
-        load_scales(nc.gpsimd, s2, w2_scales)
-        for a in (0, 2, 4):
-            load_words(w1, w1_words, a, a + 2)
-            load_words(w3, w3_words, a, a + 2)
-            if a == 0:
-                nc.sync.dma_start(out=gates[:], in_=gate)
-
+        nc.gpsimd.memset(planes[:, :, 0, :].bitcast(I32), 0)
+        nc.vector.memset(warm[:], 0.0)
+        nc.scalar.activation(warm[:], warm[:], SILU)
+        zero(nc.vector, s1[:, 1:E, :])
+        zero(nc.vector, s3[:, 1:E, :])
         nc.gpsimd.memset(scattered[:], 0.0)
 
-        def interleave(c, copy):
+        load_words(w1[:, 0:1, :], w1_words, SHARED, SHARED + 1)
+        load_scales(nc.sync, s1, w1_scales, SHARED, SHARED + 1)
+        load_words(w3[:, 0:1, :], w3_words, SHARED, SHARED + 1)
+        load_x(0)
+        load_x(1)
+        load_scales(nc.sync, s3, w3_scales, SHARED, SHARED + 1)
+        load_x(2)
+        load_x(3)
+        nc.sync.dma_start(offsets[:], offs)
+        make_identity(nc, ident[:])
+
+        def permute_words(m, words):
+            nc.vector.tensor_copy(
+                shared_w[m][:].bitcast(U16).rearrange("p (t c i) -> p c t i", t=4, i=8),
+                words[:, 0, :].bitcast(U16).rearrange("p (c i t) -> p c t i", t=4, i=8),
+            )
+
+        def permute_scales(m, plane):
+            nc.vector.tensor_copy(
+                shared_s[m][:].rearrange("p (t c i) -> p c t i", t=4, i=16),
+                plane[:, 0, :].rearrange("p (c i t) -> p c t i", t=4, i=16),
+            )
+
+        def scratch(shape, dtype, name, after):
+            if after is None:
+                return work.tile(shape, dtype, name=name, align_bytes=64)
+            return reuse.tile(shape, dtype, name=name, tag=after, align_bytes=64)
+
+        def cast_quads(c):
             quads = work.tile([P, UNIT, 4], BF16, name="quads", align_bytes=64)
-            copy(quads[:].rearrange("p (c i) j -> p c j i", i=4), raw[c][:].rearrange("p j (c i) -> p c j i", i=4))
+            nc.vector.tensor_copy(quads[:].rearrange("p (c i) j -> p c j i", i=4), raw[c][:].rearrange("p j (c i) -> p c j i", i=4))
             return quads[:].rearrange("p c j -> p (c j)")
 
-        def make_pairs(c, copy):
+        def cast_pairs(c, copy):
             copy(
-                pairs[:, :, c * 2 * UNIT : (c + 1) * 2 * UNIT].rearrange("p h (t e) -> p h t e", e=2),
+                pairs[:, :, c * UNIT : (c + 1) * UNIT].bitcast(BF16).rearrange("p h (t e) -> p h t e", e=2),
                 raw[c][:].rearrange("p (h e) t -> p h t e", e=2),
             )
 
-        def gather(u):
-            quads = work.tile([P, UNIT, 4], BF16, name="quads", align_bytes=64)
+        def weave(planes, slot=None):
+            quads = scratch([P, UNIT, 4], BF16, "quads", slot)
             flat = quads[:].rearrange("p c j -> p (c j)")
-            words = flat.bitcast(U32).rearrange("p (c h) -> p c h", h=2)
-            for h in range(2):
-                nc.vector.tensor_copy(
-                    words[:, :, h],
-                    pairs[:, h, :].bitcast(U32).indirect(offsets[:, u * UNIT // 16 : (u + 1) * UNIT // 16]),
-                )
+            nc.scalar.copy(flat.bitcast(U32).rearrange("p (t h) -> p t h", h=2), planes.rearrange("p h t -> p t h"))
             return flat
+
+        def slots(u):
+            return offsets[:, u * UNIT // 16 : (u + 1) * UNIT // 16]
+
+        def gather(u, slot=None):
+            picked = scratch([P, 2, UNIT], U32, "picked", slot)
+            for h in range(2):
+                nc.vector.tensor_copy(picked[:, h, :], pairs[:, h, :].indirect(slots(u)))
+            return picked[:]
 
         def quantize(tag, flat):
             width = flat.shape[1] // 4
@@ -118,94 +135,150 @@ def tile_moe_shr_glu_silu_kernel(tc, xT, w1_words, w1_scales, w3_words, w3_scale
             nc.vector.quantize_mx(out=codes[:].bitcast(FP8X4), scales=scales[:], in_=flat)
             return codes, scales
 
-        def finish(y, at):
-            cols = slice(at, at + y.shape[1])
-            nc.vector.tensor_tensor(result[:, cols], y[:], scattered[:, cols], ADD)
-            nc.sync.dma_start(out=out[:, cols], in_=result[:, cols])
+        def banks():
+            a = psum.tile([P, 4, P], F32, name="a", bufs=2)
+            b = psum.tile([P, 4, P], F32, name="b", bufs=4)
+            return a, b
 
-        def hidden(codes, scales, experts):
-            tiles = len(experts)
-            back = psum.tile([P, tiles, 2, P], F32, name="back")
-            for t, e in enumerate(experts):
-                cols = slice(t * P, (t + 1) * P)
-                a = psum.tile([P, H], F32, name="a")
-                b = psum.tile([P, H], F32, name="b")
-                for acc, w, s in ((a, w1, s1), (b, w3, s3)):
+        def shared_tile(xq, h, t, slot=None):
+            codes, scales = xq
+            cols = slice(t * P, (t + 1) * P)
+            a, b = banks()
+            for m, acc in enumerate((a, b)):
+                for d in range(4):
                     nc.tensor.matmul_mx(
-                        out=acc[:], lhsT=codes[:, cols].bitcast(FP8X4), lhsT_scale=scales[:, cols],
-                        rhs=w[:, e, :].bitcast(FP4X4), rhs_scale=s[:, e, :], start=True, stop=True,
+                        out=acc[:, d, :], lhsT=shared_w[m][:, 2 * d * P : 2 * (d + 1) * P].bitcast(FP4X4),
+                        lhsT_scale=shared_s[m][:, d * P : (d + 1) * P],
+                        rhs=codes[:, cols].bitcast(FP8X4), rhs_scale=scales[:, cols], start=True, stop=True,
                     )
-                act = work.tile([P, H], F32, name="act")
-                nc.scalar.activation(
-                    act[:].rearrange("p (u m e) -> p u m e", u=2, e=2),
-                    a[:].rearrange("p (m u e) -> p u m e", u=2, e=2),
-                    SILU,
+            act = scratch([P, P, 4], F32, "act", slot)
+            nc.scalar.activation(act[:], a[:].rearrange("p d n -> p n d"), SILU)
+            nc.vector.tensor_tensor(h[:, cols, :], act[:], b[:].rearrange("p d n -> p n d"), MULT)
+
+        def hidden_tile(slot=None):
+            return scratch([P, UNIT, 4], BF16, "h", slot)
+
+        def quantize_shared(c, h):
+            cols = slice(c * UNIT, (c + 1) * UNIT)
+            nc.vector.quantize_mx(
+                out=hidden_codes[:, cols].bitcast(FP8X4), scales=hidden_scales[:, cols], in_=h[:].rearrange("p c j -> p (c j)")
+            )
+
+        def shared_last(half):
+            cols = slice(half * 2 * UNIT, (half + 1) * 2 * UNIT)
+            y = psum.tile([P, 4, P], F32, name="b", bufs=4)
+            y = y[:].rearrange("p d n -> p (d n)")
+            nc.tensor.matmul_mx(
+                out=y, lhsT=w2[:, SHARED, :].bitcast(FP4X4), lhsT_scale=s2[:, SHARED, :],
+                rhs=hidden_codes[:, cols].bitcast(FP8X4), rhs_scale=hidden_scales[:, cols], start=True, stop=True,
+            )
+            return y
+
+        def routed_tile(xq, e, slot=None):
+            codes, scales = xq
+            cols = slice(e % TILES * P, (e % TILES + 1) * P)
+            a, b = (acc[:].rearrange("p d n -> p (d n)") for acc in banks())
+            for acc, w, s in ((a, w1, s1), (b, w3, s3)):
+                nc.tensor.matmul_mx(
+                    out=acc, lhsT=codes[:, cols].bitcast(FP8X4), lhsT_scale=scales[:, cols],
+                    rhs=w[:, e, :].bitcast(FP4X4), rhs_scale=s[:, e, :], start=True, stop=True,
                 )
-                h = work.tile([P, H], BF16, name="h")
-                nc.vector.tensor_tensor(
-                    h[:].rearrange("p (u m e) -> p u m e", u=2, e=2),
-                    act[:].rearrange("p (u m e) -> p u m e", u=2, e=2),
-                    b[:].rearrange("p (m u e) -> p u m e", u=2, e=2),
-                    MULT,
-                )
-                hw = h[:].bitcast(F32)
-                for u in range(2):
-                    nc.tensor.transpose(back[:, t, u, :], hw[:, u * P : (u + 1) * P], ident[:])
-            turned = work.tile([P, tiles * P, 4], BF16, name="turned", align_bytes=64)
-            flat = turned[:].rearrange("p c j -> p (c j)")
+            act = scratch([P, P, 4], F32, "act", slot)
+            act = act[:].rearrange("p n d -> p (n d)").rearrange("p (u m e) -> p u m e", u=2, e=2)
+            nc.scalar.activation(act, a.rearrange("p (m u e) -> p u m e", u=2, e=2), SILU)
+            row = work.tile([P, H], BF16, name="row")
+            nc.vector.tensor_tensor(
+                row[:].rearrange("p (u m e) -> p u m e", u=2, e=2), act,
+                b.rearrange("p (m u e) -> p u m e", u=2, e=2), MULT,
+            )
+            return row
+
+        def turn(rows):
+            back = psum.tile([P, TILES, 2, P], F32, name="back")
+            for t in range(TILES):
+                words = rows[t][:].bitcast(F32)
+                for v in range(2):
+                    nc.tensor.transpose(back[:, t, v, :], words[:, v * P : (v + 1) * P], ident[:])
+            flat = hidden_tile()[:].rearrange("p c j -> p (c j)")
             nc.scalar.copy(
-                flat.bitcast(F32).rearrange("p (t r u) -> p t r u", t=tiles, u=2),
+                flat.bitcast(F32).rearrange("p (t r u) -> p t r u", t=TILES, u=2),
                 back[:].rearrange("p t u r -> p t r u"),
             )
-            return quantize("h", flat)
+            return flat
 
-        def last(y, codes, scales, experts):
-            for t, e in enumerate(experts):
+        def routed_last(u, hq, slot=None):
+            codes, scales = hq
+            y = psum.tile([P, UNIT], F32, name="y")
+            for t in range(TILES):
+                e = u * TILES + t
                 cols = slice(t * P, (t + 1) * P)
                 nc.tensor.matmul_mx(
                     out=y[:, cols], lhsT=w2[:, e, :].bitcast(FP4X4), lhsT_scale=s2[:, e, :],
                     rhs=codes[:, cols].bitcast(FP8X4), rhs_scale=scales[:, cols], start=True, stop=True,
                 )
-
-        def shared_unit(c, copy):
-            flat = interleave(c, copy)
-            codes, scales = quantize("x", flat)
-            hc, hs = hidden(codes, scales, (SHARED,) * TILES)
-            y = psum.tile([P, UNIT], F32, name="y")
-            last(y, hc, hs, (SHARED,) * TILES)
-            return y
-
-        def routed_unit(u):
-            flat = gather(u)
-            codes, scales = quantize("x", flat)
-            experts = tuple(range(u * TILES, (u + 1) * TILES))
-            hc, hs = hidden(codes, scales, experts)
-            y = psum.tile([P, UNIT], F32, name="y")
-            last(y, hc, hs, experts)
-            ysb = work.tile([P, UNIT], F32, name="ysb")
+            ysb = scratch([P, UNIT], F32, "ysb", slot)
             nc.scalar.copy(ysb[:], y[:])
-            nc.vector.tensor_tensor(
-                scattered[:].indirect(offsets[:, u * UNIT // 16 : (u + 1) * UNIT // 16]),
-                ysb[:], gates[:, u * UNIT : (u + 1) * UNIT], MULT,
-            )
+            return ysb
 
-        y = shared_unit(0, nc.vector.tensor_copy)
-        nc.scalar.copy(early[:, 0:UNIT], y[:])
-        y = shared_unit(1, nc.scalar.copy)
-        nc.scalar.copy(early[:, UNIT : 2 * UNIT], y[:])
-        for c in range(4):
-            make_pairs(c, nc.vector.tensor_copy)
-        for u in range(3):
-            routed_unit(u)
-        half = slice(0, 2 * UNIT)
-        nc.vector.tensor_tensor(result[:, half], early[:], scattered[:, half], ADD)
-        nc.sync.dma_start(out=out[:, half], in_=result[:, half])
-        y = shared_unit(2, nc.scalar.copy)
-        finish(y, 2 * UNIT)
-        codes, scales = quantize("x", interleave(3, nc.scalar.copy))
-        for t in range(TILES):
-            cols = slice(t * P, (t + 1) * P)
-            hc, hs = hidden(codes[:, cols], scales[:, cols], (SHARED,))
-            y = psum.tile([P, P], F32, name="y")
-            last(y, hc, hs, (SHARED,))
-            finish(y, 3 * UNIT + t * P)
+        def scatter(u, ysb):
+            nc.vector.tensor_tensor(scattered[:].indirect(slots(u)), ysb[:], gates[:, u * UNIT : (u + 1) * UNIT], MULT)
+
+        def finish(y, at):
+            cols = slice(at, at + y.shape[1])
+            nc.vector.tensor_tensor(result[:, cols], y, scattered[:, cols], ADD)
+            nc.sync.dma_start(out=out[:, cols], in_=result[:, cols])
+
+        permute_words(0, w1)
+        permute_scales(0, s1)
+        permute_words(1, w3)
+        load_words(w1[:], w1_words, 0, E)
+        load_scales(nc.sync, s1, w1_scales, 0, E)
+        load_words(w3[:], w3_words, 0, E)
+        flat = cast_quads(0)
+        cast_pairs(0, nc.scalar.copy)
+        xq0 = quantize("x", flat)
+        permute_scales(1, s3)
+        load_scales(nc.sync, s3, w3_scales, 0, E)
+        flat = cast_quads(1)
+        cast_pairs(1, nc.scalar.copy)
+        load_words(w2[:], w2_words, 0, E + 1)
+        zero(nc.gpsimd, s2[:])
+        load_scales(nc.sync, s2, w2_scales, 0, E + 1)
+        xq1 = quantize("x", flat)
+        hs = [hidden_tile() for c in range(4)]
+        shared_tile(xq0, hs[0], 0)
+        cast_pairs(2, nc.scalar.copy)
+        nc.sync.dma_start(out=gates[:], in_=gate)
+        cast_pairs(3, nc.vector.tensor_copy)
+        shared_tile(xq0, hs[0], 1)
+        p0 = gather(0)
+        quantize_shared(0, hs[0])
+        shared_tile(xq1, hs[1], 0, "hold_g1")
+        r0 = quantize("x", weave(p0))
+        shared_tile(xq1, hs[1], 1)
+        p1 = gather(1, "hold_g1")
+        quantize_shared(1, hs[1])
+        xq2 = quantize("x", weave(pairs[:, :, 2 * UNIT : 3 * UNIT], "hold_g2"))
+        r1 = quantize("x", weave(p1))
+        p2 = gather(2, "hold_g2")
+        shared_tile(xq2, hs[2], 0)
+        shared_tile(xq2, hs[2], 1)
+        r2 = quantize("x", weave(p2))
+        quantize_shared(2, hs[2])
+        rows0 = [routed_tile(r0, 0), routed_tile(r0, 1, "hold_x3")]
+        rows1 = [routed_tile(r1, 2), routed_tile(r1, 3)]
+        xq3 = quantize("x", weave(pairs[:, :, 3 * UNIT : 4 * UNIT], "hold_x3"))
+        hq0 = quantize("h", turn(rows0))
+        rows2 = [routed_tile(r2, 4), routed_tile(r2, 5, "hold_y0")]
+        hq1 = quantize("h", turn(rows1))
+        y0 = routed_last(0, hq0, "hold_y0")
+        shared_tile(xq3, hs[3], 0, "hold_y1")
+        scatter(0, y0)
+        hq2 = quantize("h", turn(rows2))
+        y1 = routed_last(1, hq1, "hold_y1")
+        shared_tile(xq3, hs[3], 1)
+        scatter(1, y1)
+        quantize_shared(3, hs[3])
+        scatter(2, routed_last(2, hq2))
+        for half in range(2):
+            finish(shared_last(half), half * 2 * UNIT)

@@ -20,6 +20,7 @@ K, T, E, C, H, N = 512, 1024, 6, 128, 512, 128
 SHARED = E
 UNIT = 256
 TILES = UNIT // P
+BANK = 2048
 FLOPS = 2 * (E * C + T) * (2 * K * H + H * N)
 
 
@@ -33,25 +34,30 @@ def tile_moe_shr_glu_silu_kernel(tc, xT, w1_words, w1_scales, w3_words, w3_scale
 
         offsets = keep.tile([P, E * C // 16], U16, name="offsets")
         pairs = keep.tile([P, 2, T], U32, name="pairs", align_bytes=64)
-        w1 = keep.tile([P, E, 2 * H], U8, name="w1", align_bytes=64)
         w3 = keep.tile([P, E, 2 * H], U8, name="w3", align_bytes=64)
-        shared_w = [keep.tile([P, 2 * H], U8, name=f"shared_w{m}", align_bytes=64) for m in range(2)]
         shared_s = [keep.tile([P, H], U8, name=f"shared_s{m}", align_bytes=64) for m in range(2)]
-        planes = keep.tile([P, 2, E, H], U8, name="planes", align_bytes=64)
-        s1 = planes[:, 0]
-        s3 = planes[:, 1]
+        planes = keep.tile([P, 2 * E * H], U8, name="planes", align_bytes=64)
+        s1 = planes[:, 0 : E * H].rearrange("p (e n) -> p e n", e=E)
+        s3 = planes[:, E * H : 2 * E * H].rearrange("p (e n) -> p e n", e=E)
+        staged = [planes[:, 0:H], planes[:, E * H - H // 2 : E * H + H // 2]]
         hidden_codes = keep.tile([P, T], U32, name="hidden_codes", align_bytes=64)
         hidden_scales = keep.tile([P, T], U8, name="hidden_scales", align_bytes=64)
         scattered = keep.tile([P, T], F32, name="scattered")
         result = keep.tile([P, T], F32, name="result")
         ident = keep.tile([P, P], F32, name="ident")
 
-        warm = reuse.tile([P, 16], F32, name="warm", offset=3 * 4096 - 32)
-
-        raw = [reuse.tile([P, 4, UNIT], F32, name=f"raw{c}", offset=c * 4096, align_bytes=64) for c in range(4)]
-        w2 = reuse.tile([P, E + 1, 2 * N], U8, name="w2", offset=4096, align_bytes=64)
-        s2 = reuse.tile([P, E + 1, N], U8, name="s2", offset=6144, align_bytes=64)
-        gates = reuse.tile([P, E * C], F32, name="gates", offset=8192, align_bytes=64)
+        at = [2048, 6144, 11264, 17408]
+        warmed = reuse.tile([P, 272], F32, name="warmed", offset=at[1] + 4096 - 32)
+        shared_w = [
+            reuse.tile([P, 2 * H], U8, name="shared_w1", offset=at[1] + 4096, align_bytes=64),
+            keep.tile([P, 2 * H], U8, name="shared_w3", align_bytes=64),
+        ]
+        first1 = reuse.tile([P, 1, 2 * H], U8, name="first1", offset=at[3], align_bytes=64)
+        raw = [reuse.tile([P, 4, UNIT], F32, name=f"raw{c}", offset=at[c], align_bytes=64) for c in range(4)]
+        w1 = reuse.tile([P, E, 2 * H], U8, name="w1", offset=0, align_bytes=64)
+        w2 = reuse.tile([P, E + 1, 2 * N], U8, name="w2", offset=24576 - 1024, align_bytes=64)
+        s2 = reuse.tile([P, E + 1, N], U8, name="s2", offset=24576 + 1024, align_bytes=64)
+        gates = reuse.tile([P, E * C], F32, name="gates", offset=at[3] + 2048, align_bytes=64)
 
         def zero(eng, t):
             eng.memset(t.rearrange("p e n -> p (e n)").bitcast(I32), 0)
@@ -62,27 +68,29 @@ def tile_moe_shr_glu_silu_kernel(tc, xT, w1_words, w1_scales, w3_words, w3_scale
         def load_words(tile, words, a, b):
             nc.sync.dma_start(out=tile.bitcast(I32), in_=words[a:b, 0].bitcast(I32).rearrange("e p n -> p e n"))
 
-        def load_scales(eng, tile, scales, a, b):
+        def load_scale_rows(plane, scales, a, b, r):
             view = scales[a:b].bitcast(I32).rearrange("e s (q r) n -> r q (e s) n", r=4)
+            nc.sync.dma_start(out=plane[r:P:32].bitcast(I32), in_=view[r])
+
+        def load_scales(plane, scales, a, b):
             for r in range(4):
-                eng.dma_start(out=tile[r:P:32, 0 : b - a, :].bitcast(I32), in_=view[r])
+                load_scale_rows(plane, scales, a, b, r)
 
-        nc.gpsimd.memset(planes[:, :, 0, :].bitcast(I32), 0)
-        nc.vector.memset(warm[:], 0.0)
-        nc.scalar.activation(warm[:], warm[:], SILU)
-        zero(nc.vector, s1[:, 1:E, :])
-        zero(nc.vector, s3[:, 1:E, :])
-        nc.gpsimd.memset(scattered[:], 0.0)
+        nc.vector.memset(staged[0].bitcast(I32), 0)
+        nc.vector.memset(staged[1].bitcast(I32), 0)
+        nc.vector.memset(planes[:, E * H + H // 2 : 2 * E * H].bitcast(I32), 0)
+        nc.scalar.activation(warmed[:], planes[:, E * H - H // 2 : E * H - H // 2 + 1088].bitcast(F32), SILU)
+        nc.vector.memset(planes[:, H : E * H - H // 2].bitcast(I32), 0)
+        nc.vector.memset(scattered[:], 0.0)
 
-        load_words(w1[:, 0:1, :], w1_words, SHARED, SHARED + 1)
-        load_scales(nc.sync, s1, w1_scales, SHARED, SHARED + 1)
+        nc.sync.dma_start(offsets[:], offs)
+        load_words(first1[:], w1_words, SHARED, SHARED + 1)
         load_words(w3[:, 0:1, :], w3_words, SHARED, SHARED + 1)
         load_x(0)
+        load_scales(staged[0].rearrange("p (e n) -> p e n", e=1), w1_scales, SHARED, SHARED + 1)
         load_x(1)
-        load_scales(nc.sync, s3, w3_scales, SHARED, SHARED + 1)
         load_x(2)
-        load_x(3)
-        nc.sync.dma_start(offsets[:], offs)
+        load_scales(staged[1].rearrange("p (e n) -> p e n", e=1), w3_scales, SHARED, SHARED + 1)
         make_identity(nc, ident[:])
 
         def permute_words(m, words):
@@ -91,15 +99,17 @@ def tile_moe_shr_glu_silu_kernel(tc, xT, w1_words, w1_scales, w3_words, w3_scale
                 words[:, 0, :].bitcast(U16).rearrange("p (c i t) -> p c t i", t=4, i=8),
             )
 
-        def permute_scales(m, plane):
+        def permute_scales(m):
             nc.vector.tensor_copy(
                 shared_s[m][:].rearrange("p (t c i) -> p c t i", t=4, i=16),
-                plane[:, 0, :].rearrange("p (c i t) -> p c t i", t=4, i=16),
+                staged[m].rearrange("p (c i t) -> p c t i", t=4, i=16),
             )
 
         def scratch(shape, dtype, name, after):
             if after is None:
                 return work.tile(shape, dtype, name=name, align_bytes=64)
+            if isinstance(after, int):
+                return reuse.tile(shape, dtype, name=f"{name}_{after}", offset=after, align_bytes=64)
             return reuse.tile(shape, dtype, name=name, tag=after, align_bytes=64)
 
         def cast_quads(c):
@@ -135,15 +145,15 @@ def tile_moe_shr_glu_silu_kernel(tc, xT, w1_words, w1_scales, w3_words, w3_scale
             nc.vector.quantize_mx(out=codes[:].bitcast(FP8X4), scales=scales[:], in_=flat)
             return codes, scales
 
-        def banks():
-            a = psum.tile([P, 4, P], F32, name="a", bufs=2)
-            b = psum.tile([P, 4, P], F32, name="b", bufs=4)
+        def banks(pair):
+            a = psum.tile([P, 4, P], F32, name=f"a{pair}", offset=2 * pair * BANK)
+            b = psum.tile([P, 4, P], F32, name=f"b{pair}", offset=(2 * pair + 1) * BANK)
             return a, b
 
-        def shared_tile(xq, h, t, slot=None):
+        def shared_tile(xq, h, t, pair, slot=None):
             codes, scales = xq
             cols = slice(t * P, (t + 1) * P)
-            a, b = banks()
+            a, b = banks(pair)
             for m, acc in enumerate((a, b)):
                 for d in range(4):
                     nc.tensor.matmul_mx(
@@ -164,20 +174,19 @@ def tile_moe_shr_glu_silu_kernel(tc, xT, w1_words, w1_scales, w3_words, w3_scale
                 out=hidden_codes[:, cols].bitcast(FP8X4), scales=hidden_scales[:, cols], in_=h[:].rearrange("p c j -> p (c j)")
             )
 
-        def shared_last(half):
+        def shared_last(half, bank):
             cols = slice(half * 2 * UNIT, (half + 1) * 2 * UNIT)
-            y = psum.tile([P, 4, P], F32, name="b", bufs=4)
-            y = y[:].rearrange("p d n -> p (d n)")
+            y = psum.tile([P, 2 * UNIT], F32, name=f"ys{half}", offset=bank * BANK)[:]
             nc.tensor.matmul_mx(
                 out=y, lhsT=w2[:, SHARED, :].bitcast(FP4X4), lhsT_scale=s2[:, SHARED, :],
                 rhs=hidden_codes[:, cols].bitcast(FP8X4), rhs_scale=hidden_scales[:, cols], start=True, stop=True,
             )
             return y
 
-        def routed_tile(xq, e, slot=None):
+        def routed_tile(xq, e, pair, slot=None):
             codes, scales = xq
             cols = slice(e % TILES * P, (e % TILES + 1) * P)
-            a, b = (acc[:].rearrange("p d n -> p (d n)") for acc in banks())
+            a, b = (acc[:].rearrange("p d n -> p (d n)") for acc in banks(pair))
             for acc, w, s in ((a, w1, s1), (b, w3, s3)):
                 nc.tensor.matmul_mx(
                     out=acc, lhsT=codes[:, cols].bitcast(FP8X4), lhsT_scale=scales[:, cols],
@@ -194,7 +203,7 @@ def tile_moe_shr_glu_silu_kernel(tc, xT, w1_words, w1_scales, w3_words, w3_scale
             return row
 
         def turn(rows):
-            back = psum.tile([P, TILES, 2, P], F32, name="back")
+            back = psum.tile([P, TILES, 2, P], F32, name="back", offset=6 * BANK)
             for t in range(TILES):
                 words = rows[t][:].bitcast(F32)
                 for v in range(2):
@@ -208,7 +217,7 @@ def tile_moe_shr_glu_silu_kernel(tc, xT, w1_words, w1_scales, w3_words, w3_scale
 
         def routed_last(u, hq, slot=None):
             codes, scales = hq
-            y = psum.tile([P, UNIT], F32, name="y")
+            y = psum.tile([P, UNIT], F32, name="y", offset=7 * BANK)
             for t in range(TILES):
                 e = u * TILES + t
                 cols = slice(t * P, (t + 1) * P)
@@ -228,57 +237,61 @@ def tile_moe_shr_glu_silu_kernel(tc, xT, w1_words, w1_scales, w3_words, w3_scale
             nc.vector.tensor_tensor(result[:, cols], y, scattered[:, cols], ADD)
             nc.sync.dma_start(out=out[:, cols], in_=result[:, cols])
 
-        permute_words(0, w1)
-        permute_scales(0, s1)
+        permute_words(0, first1)
+        load_x(3)
         permute_words(1, w3)
-        load_words(w1[:], w1_words, 0, E)
-        load_scales(nc.sync, s1, w1_scales, 0, E)
         load_words(w3[:], w3_words, 0, E)
         flat = cast_quads(0)
+        permute_scales(0)
         cast_pairs(0, nc.scalar.copy)
+        load_words(w1[:], w1_words, 0, E)
         xq0 = quantize("x", flat)
-        permute_scales(1, s3)
-        load_scales(nc.sync, s3, w3_scales, 0, E)
         flat = cast_quads(1)
+        permute_scales(1)
+        for r in range(4):
+            load_scale_rows(s1, w1_scales, 0, E, r)
+            load_scale_rows(s3, w3_scales, 0, E, r)
         cast_pairs(1, nc.scalar.copy)
-        load_words(w2[:], w2_words, 0, E + 1)
-        zero(nc.gpsimd, s2[:])
-        load_scales(nc.sync, s2, w2_scales, 0, E + 1)
         xq1 = quantize("x", flat)
         hs = [hidden_tile() for c in range(4)]
-        shared_tile(xq0, hs[0], 0)
-        cast_pairs(2, nc.scalar.copy)
-        nc.sync.dma_start(out=gates[:], in_=gate)
+        cast_pairs(2, nc.vector.tensor_copy)
+        shared_tile(xq0, hs[0], 0, 0, 24576)
+        load_words(w2[:], w2_words, 0, E + 1)
+        zero(nc.gpsimd, s2[:])
+        load_scales(s2, w2_scales, 0, E + 1)
         cast_pairs(3, nc.vector.tensor_copy)
-        shared_tile(xq0, hs[0], 1)
         p0 = gather(0)
+        shared_tile(xq0, hs[0], 1, 1, at[3] + 2048)
+        nc.sync.dma_start(out=gates[:], in_=gate)
         quantize_shared(0, hs[0])
-        shared_tile(xq1, hs[1], 0, "hold_g1")
+        shared_tile(xq1, hs[1], 0, 0, at[3])
         r0 = quantize("x", weave(p0))
-        shared_tile(xq1, hs[1], 1)
-        p1 = gather(1, "hold_g1")
+        shared_tile(xq1, hs[1], 1, 1)
+        p1 = gather(1, at[3])
         quantize_shared(1, hs[1])
         xq2 = quantize("x", weave(pairs[:, :, 2 * UNIT : 3 * UNIT], "hold_g2"))
         r1 = quantize("x", weave(p1))
         p2 = gather(2, "hold_g2")
-        shared_tile(xq2, hs[2], 0)
-        shared_tile(xq2, hs[2], 1)
+        shared_tile(xq2, hs[2], 0, 2)
+        shared_tile(xq2, hs[2], 1, 3)
         r2 = quantize("x", weave(p2))
         quantize_shared(2, hs[2])
-        rows0 = [routed_tile(r0, 0), routed_tile(r0, 1, "hold_x3")]
-        rows1 = [routed_tile(r1, 2), routed_tile(r1, 3)]
+        rows0 = [routed_tile(r0, 0, 0), routed_tile(r0, 1, 1, "hold_x3")]
+        rows1 = [routed_tile(r1, 2, 2), routed_tile(r1, 3, 0)]
         xq3 = quantize("x", weave(pairs[:, :, 3 * UNIT : 4 * UNIT], "hold_x3"))
         hq0 = quantize("h", turn(rows0))
-        rows2 = [routed_tile(r2, 4), routed_tile(r2, 5, "hold_y0")]
+        rows2 = [routed_tile(r2, 4, 1), routed_tile(r2, 5, 2, "hold_y0")]
         hq1 = quantize("h", turn(rows1))
         y0 = routed_last(0, hq0, "hold_y0")
-        shared_tile(xq3, hs[3], 0, "hold_y1")
+        shared_tile(xq3, hs[3], 0, 0, "hold_y1")
         scatter(0, y0)
         hq2 = quantize("h", turn(rows2))
         y1 = routed_last(1, hq1, "hold_y1")
-        shared_tile(xq3, hs[3], 1)
+        shared_tile(xq3, hs[3], 1, 1)
         scatter(1, y1)
         quantize_shared(3, hs[3])
         scatter(2, routed_last(2, hq2))
-        for half in range(2):
-            finish(shared_last(half), half * 2 * UNIT)
+        finish(shared_last(0, 6), 0)
+        y = shared_last(1, 4)
+        finish(y[:, 0:UNIT], 2 * UNIT)
+        finish(y[:, UNIT : 2 * UNIT], 3 * UNIT)

@@ -36,10 +36,11 @@ def tile_moe_shr_glu_silu_kernel(tc, xT, w1_words, w1_scales, w3_words, w3_scale
         pairs = keep.tile([P, 2, T], U32, name="pairs", align_bytes=64)
         w3 = keep.tile([P, E, 2 * H], U8, name="w3", align_bytes=64)
         shared_s = [keep.tile([P, H], U8, name=f"shared_s{m}", align_bytes=64) for m in range(2)]
-        planes = keep.tile([P, 2 * E * H], U8, name="planes", align_bytes=64)
+        planes = keep.tile([P, 2 * E * H + (E + 1) * N], U8, name="planes", align_bytes=64)
         s1 = planes[:, 0 : E * H].rearrange("p (e n) -> p e n", e=E)
         s3 = planes[:, E * H : 2 * E * H].rearrange("p (e n) -> p e n", e=E)
-        staged = [planes[:, 0:H], planes[:, E * H - H // 2 : E * H + H // 2]]
+        s2 = planes[:, 2 * E * H :].rearrange("p (e n) -> p e n", e=E + 1)
+        staged = [planes[:, 2 * E * H : 2 * E * H + H], planes[:, E * H - H // 2 : E * H + H // 2]]
         hidden_codes = keep.tile([P, T], U32, name="hidden_codes", align_bytes=64)
         hidden_scales = keep.tile([P, T], U8, name="hidden_scales", align_bytes=64)
         scattered = keep.tile([P, T], F32, name="scattered")
@@ -56,11 +57,7 @@ def tile_moe_shr_glu_silu_kernel(tc, xT, w1_words, w1_scales, w3_words, w3_scale
         raw = [reuse.tile([P, 4, UNIT], F32, name=f"raw{c}", offset=at[c], align_bytes=64) for c in range(4)]
         w1 = reuse.tile([P, E, 2 * H], U8, name="w1", offset=0, align_bytes=64)
         w2 = reuse.tile([P, E + 1, 2 * N], U8, name="w2", offset=24576 - 1024, align_bytes=64)
-        s2 = reuse.tile([P, E + 1, N], U8, name="s2", offset=24576 + 1024, align_bytes=64)
-        gates = reuse.tile([P, E * C], F32, name="gates", offset=at[3] + 2048, align_bytes=64)
-
-        def zero(eng, t):
-            eng.memset(t.rearrange("p e n -> p (e n)").bitcast(I32), 0)
+        gates = reuse.tile([P, E * C], F32, name="gates", offset=at[3] + 2112, align_bytes=64)
 
         def load_x(c):
             nc.sync.dma_start(out=raw[c][:], in_=xT.rearrange("(p j) t -> p j t", j=4)[:, :, c * UNIT : (c + 1) * UNIT])
@@ -80,7 +77,8 @@ def tile_moe_shr_glu_silu_kernel(tc, xT, w1_words, w1_scales, w3_words, w3_scale
         nc.vector.memset(staged[1].bitcast(I32), 0)
         nc.vector.memset(planes[:, E * H + H // 2 : 2 * E * H].bitcast(I32), 0)
         nc.scalar.activation(warmed[:], planes[:, E * H - H // 2 : E * H - H // 2 + 1088].bitcast(F32), SILU)
-        nc.vector.memset(planes[:, H : E * H - H // 2].bitcast(I32), 0)
+        nc.vector.memset(planes[:, 2 * E * H + H :].bitcast(I32), 0)
+        nc.vector.memset(planes[:, 0 : E * H - H // 2].bitcast(I32), 0)
         nc.vector.memset(scattered[:], 0.0)
 
         nc.sync.dma_start(offsets[:], offs)
@@ -232,9 +230,9 @@ def tile_moe_shr_glu_silu_kernel(tc, xT, w1_words, w1_scales, w3_words, w3_scale
         def scatter(u, ysb):
             nc.vector.tensor_tensor(scattered[:].indirect(slots(u)), ysb[:], gates[:, u * UNIT : (u + 1) * UNIT], MULT)
 
-        def finish(y, at):
+        def finish(engine, y, at):
             cols = slice(at, at + y.shape[1])
-            nc.vector.tensor_tensor(result[:, cols], y, scattered[:, cols], ADD)
+            engine.tensor_tensor(result[:, cols], y, scattered[:, cols], ADD)
             nc.sync.dma_start(out=out[:, cols], in_=result[:, cols])
 
         permute_words(0, first1)
@@ -244,6 +242,7 @@ def tile_moe_shr_glu_silu_kernel(tc, xT, w1_words, w1_scales, w3_words, w3_scale
         flat = cast_quads(0)
         permute_scales(0)
         cast_pairs(0, nc.scalar.copy)
+        load_scales(s2, w2_scales, 0, E + 1)
         load_words(w1[:], w1_words, 0, E)
         xq0 = quantize("x", flat)
         flat = cast_quads(1)
@@ -253,21 +252,19 @@ def tile_moe_shr_glu_silu_kernel(tc, xT, w1_words, w1_scales, w3_words, w3_scale
             load_scale_rows(s3, w3_scales, 0, E, r)
         cast_pairs(1, nc.scalar.copy)
         xq1 = quantize("x", flat)
-        hs = [hidden_tile() for c in range(4)]
+        hs = [hidden_tile(at[3] + 64 - 2048), hidden_tile(), hidden_tile(), hidden_tile()]
         cast_pairs(2, nc.vector.tensor_copy)
-        shared_tile(xq0, hs[0], 0, 0, 24576)
-        load_words(w2[:], w2_words, 0, E + 1)
-        zero(nc.gpsimd, s2[:])
-        load_scales(s2, w2_scales, 0, E + 1)
         cast_pairs(3, nc.vector.tensor_copy)
         p0 = gather(0)
-        shared_tile(xq0, hs[0], 1, 1, at[3] + 2048)
+        shared_tile(xq0, hs[0], 0, 0, 24576)
+        load_words(w2[:], w2_words, 0, E + 1)
+        shared_tile(xq0, hs[0], 1, 1, at[3] + 2112)
         nc.sync.dma_start(out=gates[:], in_=gate)
-        quantize_shared(0, hs[0])
-        shared_tile(xq1, hs[1], 0, 0, at[3])
         r0 = quantize("x", weave(p0))
+        quantize_shared(0, hs[0])
+        shared_tile(xq1, hs[1], 0, 0, at[3] + 64)
         shared_tile(xq1, hs[1], 1, 1)
-        p1 = gather(1, at[3])
+        p1 = gather(1, at[3] + 64)
         quantize_shared(1, hs[1])
         xq2 = quantize("x", weave(pairs[:, :, 2 * UNIT : 3 * UNIT], "hold_g2"))
         r1 = quantize("x", weave(p1))
@@ -291,7 +288,9 @@ def tile_moe_shr_glu_silu_kernel(tc, xT, w1_words, w1_scales, w3_words, w3_scale
         scatter(1, y1)
         quantize_shared(3, hs[3])
         scatter(2, routed_last(2, hq2))
-        finish(shared_last(0, 6), 0)
-        y = shared_last(1, 4)
-        finish(y[:, 0:UNIT], 2 * UNIT)
-        finish(y[:, UNIT : 2 * UNIT], 3 * UNIT)
+        early = shared_last(0, 6)
+        parked = keep.tile([P, UNIT], F32, name="parked")
+        nc.scalar.copy(parked[:], early[:, 0:UNIT])
+        finish(nc.gpsimd, parked[:], 0)
+        finish(nc.vector, shared_last(1, 4), 2 * UNIT)
+        finish(nc.vector, early[:, UNIT : 2 * UNIT], UNIT)

@@ -21,7 +21,25 @@ SHARED = E
 UNIT = 256
 TILES = UNIT // P
 BANK = 2048
+TURN_BANK, ROUTED_BANK = 6, 7
+WORK_BUFS = 7
 FLOPS = 2 * (E * C + T) * (2 * K * H + H * N)
+
+X_BYTES = 4 * UNIT * 4
+BUFFER = 2048
+EDGE = 64
+W1_AT = 0
+X0_AT = E * 2 * H - X_BYTES
+X1_AT = X0_AT + X_BYTES
+SHARED_W1_AT = X1_AT + X_BYTES
+X2_AT = SHARED_W1_AT + 2 * H
+H0_AT = X2_AT + X_BYTES + EDGE
+X3_AT = H0_AT + BUFFER - EDGE
+SILU_1A_AT = X3_AT + EDGE
+SILU_0B_AT = SILU_1A_AT + BUFFER
+SILU_0A_AT = 12 * BUFFER
+W2_AT = SILU_0A_AT - BUFFER // 2
+ZEROS = (2 * H + EDGE) // 4
 
 
 def tile_moe_shr_glu_silu_kernel(tc, xT, w1_words, w1_scales, w3_words, w3_scales, w2_words, w2_scales, gate, offs, out):
@@ -29,7 +47,7 @@ def tile_moe_shr_glu_silu_kernel(tc, xT, w1_words, w1_scales, w3_words, w3_scale
     with ExitStack() as ctx:
         keep = ctx.enter_context(tc.tile_pool(name="keep", bufs=1))
         reuse = ctx.enter_context(tc.tile_pool(name="reuse", bufs=1))
-        work = ctx.enter_context(tc.tile_pool(name="work", bufs=7))
+        work = ctx.enter_context(tc.tile_pool(name="work", bufs=WORK_BUFS))
         psum = ctx.enter_context(tc.psum_pool(name="psum", bufs=1))
 
         offsets = keep.tile([P, E * C // 16], U16, name="offsets")
@@ -47,17 +65,19 @@ def tile_moe_shr_glu_silu_kernel(tc, xT, w1_words, w1_scales, w3_words, w3_scale
         result = keep.tile([P, T], F32, name="result")
         ident = keep.tile([P, P], F32, name="ident")
 
-        at = [2048, 6144, 11264, 17408]
-        warmed = reuse.tile([P, 272], F32, name="warmed", offset=at[1] + 4096 - 32)
+        zeros = reuse.tile([P, ZEROS], F32, name="zeros", offset=SHARED_W1_AT - EDGE // 2)
         shared_w = [
-            reuse.tile([P, 2 * H], U8, name="shared_w1", offset=at[1] + 4096, align_bytes=64),
+            reuse.tile([P, 2 * H], U8, name="shared_w1", offset=SHARED_W1_AT, align_bytes=64),
             keep.tile([P, 2 * H], U8, name="shared_w3", align_bytes=64),
         ]
-        first1 = reuse.tile([P, 1, 2 * H], U8, name="first1", offset=at[3], align_bytes=64)
-        raw = [reuse.tile([P, 4, UNIT], F32, name=f"raw{c}", offset=at[c], align_bytes=64) for c in range(4)]
-        w1 = reuse.tile([P, E, 2 * H], U8, name="w1", offset=0, align_bytes=64)
-        w2 = reuse.tile([P, E + 1, 2 * N], U8, name="w2", offset=24576 - 1024, align_bytes=64)
-        gates = reuse.tile([P, E * C], F32, name="gates", offset=at[3] + 2112, align_bytes=64)
+        first1 = reuse.tile([P, 1, 2 * H], U8, name="first1", offset=X3_AT, align_bytes=64)
+        raw = [
+            reuse.tile([P, 4, UNIT], F32, name=f"raw{c}", offset=at, align_bytes=64)
+            for c, at in enumerate((X0_AT, X1_AT, X2_AT, X3_AT))
+        ]
+        w1 = reuse.tile([P, E, 2 * H], U8, name="w1", offset=W1_AT, align_bytes=64)
+        w2 = reuse.tile([P, E + 1, 2 * N], U8, name="w2", offset=W2_AT, align_bytes=64)
+        gates = reuse.tile([P, E * C], F32, name="gates", offset=SILU_0B_AT, align_bytes=64)
 
         def load_x(c):
             nc.sync.dma_start(out=raw[c][:], in_=xT.rearrange("(p j) t -> p j t", j=4)[:, :, c * UNIT : (c + 1) * UNIT])
@@ -75,11 +95,12 @@ def tile_moe_shr_glu_silu_kernel(tc, xT, w1_words, w1_scales, w3_words, w3_scale
 
         nc.vector.memset(staged[0].bitcast(I32), 0)
         nc.vector.memset(staged[1].bitcast(I32), 0)
+        nc.vector.memset(zeros[:], 0.0)
+        nc.scalar.activation(scattered[:, 0:ZEROS], zeros[:], SILU, bias=staged[1][:, 0:4].bitcast(F32))
         nc.vector.memset(planes[:, E * H + H // 2 : 2 * E * H].bitcast(I32), 0)
-        nc.scalar.activation(warmed[:], planes[:, E * H - H // 2 : E * H - H // 2 + 1088].bitcast(F32), SILU)
         nc.vector.memset(planes[:, 2 * E * H + H :].bitcast(I32), 0)
         nc.vector.memset(planes[:, 0 : E * H - H // 2].bitcast(I32), 0)
-        nc.vector.memset(scattered[:], 0.0)
+        nc.vector.memset(scattered[:, ZEROS:], 0.0)
 
         nc.sync.dma_start(offsets[:], offs)
         load_words(first1[:], w1_words, SHARED, SHARED + 1)
@@ -91,24 +112,24 @@ def tile_moe_shr_glu_silu_kernel(tc, xT, w1_words, w1_scales, w3_words, w3_scale
         load_scales(staged[1].rearrange("p (e n) -> p e n", e=1), w3_scales, SHARED, SHARED + 1)
         make_identity(nc, ident[:])
 
-        def permute_words(m, words):
+        def permute_words(matrix, words):
             nc.vector.tensor_copy(
-                shared_w[m][:].bitcast(U16).rearrange("p (t c i) -> p c t i", t=4, i=8),
-                words[:, 0, :].bitcast(U16).rearrange("p (c i t) -> p c t i", t=4, i=8),
+                shared_w[matrix][:].bitcast(U16).rearrange("p (d c i) -> p c d i", d=4, i=8),
+                words[:, 0, :].bitcast(U16).rearrange("p (c i d) -> p c d i", d=4, i=8),
             )
 
-        def permute_scales(m):
+        def permute_scales(matrix):
             nc.vector.tensor_copy(
-                shared_s[m][:].rearrange("p (t c i) -> p c t i", t=4, i=16),
-                staged[m].rearrange("p (c i t) -> p c t i", t=4, i=16),
+                shared_s[matrix][:].rearrange("p (d c i) -> p c d i", d=4, i=16),
+                staged[matrix].rearrange("p (c i d) -> p c d i", d=4, i=16),
             )
 
-        def scratch(shape, dtype, name, after):
-            if after is None:
+        def scratch(shape, dtype, name, place):
+            if place is None:
                 return work.tile(shape, dtype, name=name, align_bytes=64)
-            if isinstance(after, int):
-                return reuse.tile(shape, dtype, name=f"{name}_{after}", offset=after, align_bytes=64)
-            return reuse.tile(shape, dtype, name=name, tag=after, align_bytes=64)
+            if isinstance(place, int):
+                return reuse.tile(shape, dtype, name=f"{name}_{place}", offset=place, align_bytes=64)
+            return reuse.tile(shape, dtype, name=name, tag=place, align_bytes=64)
 
         def cast_quads(c):
             quads = work.tile([P, UNIT, 4], BF16, name="quads", align_bytes=64)
@@ -121,50 +142,49 @@ def tile_moe_shr_glu_silu_kernel(tc, xT, w1_words, w1_scales, w3_words, w3_scale
                 raw[c][:].rearrange("p (h e) t -> p h t e", e=2),
             )
 
-        def weave(planes, slot=None):
-            quads = scratch([P, UNIT, 4], BF16, "quads", slot)
+        def weave(halves, place=None):
+            quads = scratch([P, UNIT, 4], BF16, "quads", place)
             flat = quads[:].rearrange("p c j -> p (c j)")
-            nc.scalar.copy(flat.bitcast(U32).rearrange("p (t h) -> p t h", h=2), planes.rearrange("p h t -> p t h"))
+            nc.scalar.copy(flat.bitcast(U32).rearrange("p (t h) -> p t h", h=2), halves.rearrange("p h t -> p t h"))
             return flat
 
         def slots(u):
             return offsets[:, u * UNIT // 16 : (u + 1) * UNIT // 16]
 
-        def gather(u, slot=None):
-            picked = scratch([P, 2, UNIT], U32, "picked", slot)
-            for h in range(2):
-                nc.vector.tensor_copy(picked[:, h, :], pairs[:, h, :].indirect(slots(u)))
+        def gather(u, place=None):
+            picked = scratch([P, 2, UNIT], U32, "picked", place)
+            for half in range(2):
+                nc.vector.tensor_copy(picked[:, half, :], pairs[:, half, :].indirect(slots(u)))
             return picked[:]
 
         def quantize(tag, flat):
-            width = flat.shape[1] // 4
-            codes = work.tile([P, width], U32, name=tag + "_codes", align_bytes=64)
-            scales = work.tile([P, width], U8, name=tag + "_scales", align_bytes=64)
+            codes = work.tile([P, UNIT], U32, name=tag + "_codes", align_bytes=64)
+            scales = work.tile([P, UNIT], U8, name=tag + "_scales", align_bytes=64)
             nc.vector.quantize_mx(out=codes[:].bitcast(FP8X4), scales=scales[:], in_=flat)
             return codes, scales
 
-        def banks(pair):
+        def sum_banks(pair):
             a = psum.tile([P, 4, P], F32, name=f"a{pair}", offset=2 * pair * BANK)
             b = psum.tile([P, 4, P], F32, name=f"b{pair}", offset=(2 * pair + 1) * BANK)
             return a, b
 
-        def shared_tile(xq, h, t, pair, slot=None):
+        def shared_tile(xq, h, t, pair, place=None):
             codes, scales = xq
             cols = slice(t * P, (t + 1) * P)
-            a, b = banks(pair)
-            for m, acc in enumerate((a, b)):
+            a, b = sum_banks(pair)
+            for matrix, acc in enumerate((a, b)):
                 for d in range(4):
                     nc.tensor.matmul_mx(
-                        out=acc[:, d, :], lhsT=shared_w[m][:, 2 * d * P : 2 * (d + 1) * P].bitcast(FP4X4),
-                        lhsT_scale=shared_s[m][:, d * P : (d + 1) * P],
+                        out=acc[:, d, :], lhsT=shared_w[matrix][:, 2 * d * P : 2 * (d + 1) * P].bitcast(FP4X4),
+                        lhsT_scale=shared_s[matrix][:, d * P : (d + 1) * P],
                         rhs=codes[:, cols].bitcast(FP8X4), rhs_scale=scales[:, cols], start=True, stop=True,
                     )
-            act = scratch([P, P, 4], F32, "act", slot)
+            act = scratch([P, P, 4], F32, "act", place)
             nc.scalar.activation(act[:], a[:].rearrange("p d n -> p n d"), SILU)
             nc.vector.tensor_tensor(h[:, cols, :], act[:], b[:].rearrange("p d n -> p n d"), MULT)
 
-        def hidden_tile(slot=None):
-            return scratch([P, UNIT, 4], BF16, "h", slot)
+        def hidden_tile(place=None):
+            return scratch([P, UNIT, 4], BF16, "h", place)
 
         def quantize_shared(c, h):
             cols = slice(c * UNIT, (c + 1) * UNIT)
@@ -174,38 +194,38 @@ def tile_moe_shr_glu_silu_kernel(tc, xT, w1_words, w1_scales, w3_words, w3_scale
 
         def shared_last(half, bank):
             cols = slice(half * 2 * UNIT, (half + 1) * 2 * UNIT)
-            y = psum.tile([P, 2 * UNIT], F32, name=f"ys{half}", offset=bank * BANK)[:]
+            ys = psum.tile([P, 2 * UNIT], F32, name=f"ys{half}", offset=bank * BANK)[:]
             nc.tensor.matmul_mx(
-                out=y, lhsT=w2[:, SHARED, :].bitcast(FP4X4), lhsT_scale=s2[:, SHARED, :],
+                out=ys, lhsT=w2[:, SHARED, :].bitcast(FP4X4), lhsT_scale=s2[:, SHARED, :],
                 rhs=hidden_codes[:, cols].bitcast(FP8X4), rhs_scale=hidden_scales[:, cols], start=True, stop=True,
             )
-            return y
+            return ys
 
-        def routed_tile(xq, e, pair, slot=None):
+        def routed_tile(xq, e, pair, place=None):
             codes, scales = xq
             cols = slice(e % TILES * P, (e % TILES + 1) * P)
-            a, b = (acc[:].rearrange("p d n -> p (d n)") for acc in banks(pair))
+            a, b = (acc[:].rearrange("p d n -> p (d n)") for acc in sum_banks(pair))
             for acc, w, s in ((a, w1, s1), (b, w3, s3)):
                 nc.tensor.matmul_mx(
                     out=acc, lhsT=codes[:, cols].bitcast(FP8X4), lhsT_scale=scales[:, cols],
                     rhs=w[:, e, :].bitcast(FP4X4), rhs_scale=s[:, e, :], start=True, stop=True,
                 )
-            act = scratch([P, P, 4], F32, "act", slot)
-            act = act[:].rearrange("p n d -> p (n d)").rearrange("p (u m e) -> p u m e", u=2, e=2)
-            nc.scalar.activation(act, a.rearrange("p (m u e) -> p u m e", u=2, e=2), SILU)
+            act = scratch([P, P, 4], F32, "act", place)
+            act = act[:].rearrange("p n d -> p (n d)").rearrange("p (u m v) -> p u m v", u=2, v=2)
+            nc.scalar.activation(act, a.rearrange("p (m u v) -> p u m v", u=2, v=2), SILU)
             row = work.tile([P, H], BF16, name="row")
             nc.vector.tensor_tensor(
-                row[:].rearrange("p (u m e) -> p u m e", u=2, e=2), act,
-                b.rearrange("p (m u e) -> p u m e", u=2, e=2), MULT,
+                row[:].rearrange("p (u m v) -> p u m v", u=2, v=2), act,
+                b.rearrange("p (m u v) -> p u m v", u=2, v=2), MULT,
             )
             return row
 
         def turn(rows):
-            back = psum.tile([P, TILES, 2, P], F32, name="back", offset=6 * BANK)
+            back = psum.tile([P, TILES, 2, P], F32, name="back", offset=TURN_BANK * BANK)
             for t in range(TILES):
                 words = rows[t][:].bitcast(F32)
-                for v in range(2):
-                    nc.tensor.transpose(back[:, t, v, :], words[:, v * P : (v + 1) * P], ident[:])
+                for u in range(2):
+                    nc.tensor.transpose(back[:, t, u, :], words[:, u * P : (u + 1) * P], ident[:])
             flat = hidden_tile()[:].rearrange("p c j -> p (c j)")
             nc.scalar.copy(
                 flat.bitcast(F32).rearrange("p (t r u) -> p t r u", t=TILES, u=2),
@@ -213,26 +233,26 @@ def tile_moe_shr_glu_silu_kernel(tc, xT, w1_words, w1_scales, w3_words, w3_scale
             )
             return flat
 
-        def routed_last(u, hq, slot=None):
+        def routed_last(unit, hq, place=None):
             codes, scales = hq
-            y = psum.tile([P, UNIT], F32, name="y", offset=7 * BANK)
+            y = psum.tile([P, UNIT], F32, name="y", offset=ROUTED_BANK * BANK)
             for t in range(TILES):
-                e = u * TILES + t
+                e = unit * TILES + t
                 cols = slice(t * P, (t + 1) * P)
                 nc.tensor.matmul_mx(
                     out=y[:, cols], lhsT=w2[:, e, :].bitcast(FP4X4), lhsT_scale=s2[:, e, :],
                     rhs=codes[:, cols].bitcast(FP8X4), rhs_scale=scales[:, cols], start=True, stop=True,
                 )
-            ysb = scratch([P, UNIT], F32, "ysb", slot)
+            ysb = scratch([P, UNIT], F32, "ysb", place)
             nc.scalar.copy(ysb[:], y[:])
             return ysb
 
-        def scatter(u, ysb):
-            nc.vector.tensor_tensor(scattered[:].indirect(slots(u)), ysb[:], gates[:, u * UNIT : (u + 1) * UNIT], MULT)
+        def scatter(unit, ysb):
+            nc.vector.tensor_tensor(scattered[:].indirect(slots(unit)), ysb[:], gates[:, unit * UNIT : (unit + 1) * UNIT], MULT)
 
-        def finish(engine, y, at):
-            cols = slice(at, at + y.shape[1])
-            engine.tensor_tensor(result[:, cols], y, scattered[:, cols], ADD)
+        def finish(engine, ys, at):
+            cols = slice(at, at + ys.shape[1])
+            engine.tensor_tensor(result[:, cols], ys, scattered[:, cols], ADD)
             nc.sync.dma_start(out=out[:, cols], in_=result[:, cols])
 
         permute_words(0, first1)
@@ -252,45 +272,48 @@ def tile_moe_shr_glu_silu_kernel(tc, xT, w1_words, w1_scales, w3_words, w3_scale
             load_scale_rows(s3, w3_scales, 0, E, r)
         cast_pairs(1, nc.scalar.copy)
         xq1 = quantize("x", flat)
-        hs = [hidden_tile(at[3] + 64 - 2048), hidden_tile(), hidden_tile(), hidden_tile()]
+        hs = [hidden_tile(H0_AT), hidden_tile(), hidden_tile(), hidden_tile()]
         cast_pairs(2, nc.vector.tensor_copy)
         cast_pairs(3, nc.vector.tensor_copy)
+
         p0 = gather(0)
-        shared_tile(xq0, hs[0], 0, 0, 24576)
+        shared_tile(xq0, hs[0], 0, 0, SILU_0A_AT)
         load_words(w2[:], w2_words, 0, E + 1)
-        shared_tile(xq0, hs[0], 1, 1, at[3] + 2112)
+        shared_tile(xq0, hs[0], 1, 1, SILU_0B_AT)
         nc.sync.dma_start(out=gates[:], in_=gate)
         r0 = quantize("x", weave(p0))
         quantize_shared(0, hs[0])
-        shared_tile(xq1, hs[1], 0, 0, at[3] + 64)
+        shared_tile(xq1, hs[1], 0, 0, SILU_1A_AT)
         shared_tile(xq1, hs[1], 1, 1)
-        p1 = gather(1, at[3] + 64)
+        p1 = gather(1, SILU_1A_AT)
         quantize_shared(1, hs[1])
-        xq2 = quantize("x", weave(pairs[:, :, 2 * UNIT : 3 * UNIT], "hold_g2"))
+        xq2 = quantize("x", weave(pairs[:, :, 2 * UNIT : 3 * UNIT], "before_last_gather"))
         r1 = quantize("x", weave(p1))
-        p2 = gather(2, "hold_g2")
+        p2 = gather(2, "before_last_gather")
         shared_tile(xq2, hs[2], 0, 2)
         shared_tile(xq2, hs[2], 1, 3)
         r2 = quantize("x", weave(p2))
         quantize_shared(2, hs[2])
-        rows0 = [routed_tile(r0, 0, 0), routed_tile(r0, 1, 1, "hold_x3")]
+
+        rows0 = [routed_tile(r0, 0, 0), routed_tile(r0, 1, 1, "before_last_unit")]
         rows1 = [routed_tile(r1, 2, 2), routed_tile(r1, 3, 0)]
-        xq3 = quantize("x", weave(pairs[:, :, 3 * UNIT : 4 * UNIT], "hold_x3"))
+        xq3 = quantize("x", weave(pairs[:, :, 3 * UNIT : 4 * UNIT], "before_last_unit"))
         hq0 = quantize("h", turn(rows0))
-        rows2 = [routed_tile(r2, 4, 1), routed_tile(r2, 5, 2, "hold_y0")]
+        rows2 = [routed_tile(r2, 4, 1), routed_tile(r2, 5, 2, "before_scatter0")]
         hq1 = quantize("h", turn(rows1))
-        y0 = routed_last(0, hq0, "hold_y0")
-        shared_tile(xq3, hs[3], 0, 0, "hold_y1")
+        y0 = routed_last(0, hq0, "before_scatter0")
+        shared_tile(xq3, hs[3], 0, 0, "before_scatter1")
         scatter(0, y0)
         hq2 = quantize("h", turn(rows2))
-        y1 = routed_last(1, hq1, "hold_y1")
+        y1 = routed_last(1, hq1, "before_scatter1")
         shared_tile(xq3, hs[3], 1, 1)
         scatter(1, y1)
         quantize_shared(3, hs[3])
         scatter(2, routed_last(2, hq2))
-        early = shared_last(0, 6)
+
+        early = shared_last(0, TURN_BANK)
         parked = keep.tile([P, UNIT], F32, name="parked")
         nc.scalar.copy(parked[:], early[:, 0:UNIT])
         finish(nc.gpsimd, parked[:], 0)
-        finish(nc.vector, shared_last(1, 4), 2 * UNIT)
+        finish(nc.vector, shared_last(1, 2 * 2), 2 * UNIT)
         finish(nc.vector, early[:, UNIT : 2 * UNIT], UNIT)

@@ -250,9 +250,9 @@ def tile_moe_shr_glu_silu_kernel(tc, xT, w1_words, w1_scales, w3_words, w3_scale
         def scatter(unit, ysb):
             nc.vector.tensor_tensor(scattered[:].indirect(slots(unit)), ysb[:], gates[:, unit * UNIT : (unit + 1) * UNIT], MULT)
 
-        def finish(engine, ys, at):
+        def finish(ys, at):
             cols = slice(at, at + ys.shape[1])
-            engine.tensor_tensor(result[:, cols], ys, scattered[:, cols], ADD)
+            nc.vector.tensor_tensor(result[:, cols], ys, scattered[:, cols], ADD)
             nc.sync.dma_start(out=out[:, cols], in_=result[:, cols])
 
         permute_words(0, first1)
@@ -311,9 +311,7 @@ def tile_moe_shr_glu_silu_kernel(tc, xT, w1_words, w1_scales, w3_words, w3_scale
         quantize_shared(3, hs[3])
         scatter(2, routed_last(2, hq2))
 
-        early = shared_last(0, TURN_BANK)
-        parked = keep.tile([P, UNIT], F32, name="parked")
-        nc.scalar.copy(parked[:], early[:, 0:UNIT])
-        finish(nc.gpsimd, parked[:], 0)
-        finish(nc.vector, shared_last(1, 2 * 2), 2 * UNIT)
-        finish(nc.vector, early[:, UNIT : 2 * UNIT], UNIT)
+        finish(shared_last(0, TURN_BANK), 0)
+        late = shared_last(1, 2 * 2)
+        finish(late[:, 0:UNIT], 2 * UNIT)
+        finish(late[:, UNIT : 2 * UNIT], 3 * UNIT)

@@ -59,8 +59,6 @@ def tile_moe_shr_glu_silu_kernel(tc, xT, w1_words, w1_scales, w3_words, w3_scale
         s3 = planes[:, E * H : 2 * E * H].rearrange("p (e n) -> p e n", e=E)
         s2 = planes[:, 2 * E * H :].rearrange("p (e n) -> p e n", e=E + 1)
         staged = [planes[:, 2 * E * H : 2 * E * H + H], planes[:, E * H - H // 2 : E * H + H // 2]]
-        hidden_codes = keep.tile([P, T], U32, name="hidden_codes", align_bytes=64)
-        hidden_scales = keep.tile([P, T], U8, name="hidden_scales", align_bytes=64)
         scattered = keep.tile([P, T], F32, name="scattered")
         result = keep.tile([P, T], F32, name="result")
         ident = keep.tile([P, P], F32, name="ident")
@@ -157,8 +155,8 @@ def tile_moe_shr_glu_silu_kernel(tc, xT, w1_words, w1_scales, w3_words, w3_scale
                 nc.vector.tensor_copy(picked[:, half, :], pairs[:, half, :].indirect(slots(u)))
             return picked[:]
 
-        def quantize(tag, flat):
-            codes = work.tile([P, UNIT], U32, name=tag + "_codes", align_bytes=64)
+        def quantize(tag, flat, place=None):
+            codes = scratch([P, UNIT], U32, tag + "_codes", place)
             scales = work.tile([P, UNIT], U8, name=tag + "_scales", align_bytes=64)
             nc.vector.quantize_mx(out=codes[:].bitcast(FP8X4), scales=scales[:], in_=flat)
             return codes, scales
@@ -183,23 +181,40 @@ def tile_moe_shr_glu_silu_kernel(tc, xT, w1_words, w1_scales, w3_words, w3_scale
             nc.scalar.activation(act[:], a[:].rearrange("p d n -> p n d"), SILU)
             nc.vector.tensor_tensor(h[:, cols, :], act[:], b[:].rearrange("p d n -> p n d"), MULT)
 
+        def shared_tile_aside(xq, t, pair):
+            codes, scales = xq
+            cols = slice(t * P, (t + 1) * P)
+            a, b = sum_banks(pair)
+            for matrix, acc in enumerate((a, b)):
+                for d in range(4):
+                    nc.tensor.matmul_mx(
+                        out=acc[:, d, :], lhsT=shared_w[matrix][:, 2 * d * P : 2 * (d + 1) * P].bitcast(FP4X4),
+                        lhsT_scale=shared_s[matrix][:, d * P : (d + 1) * P],
+                        rhs=codes[:, cols].bitcast(FP8X4), rhs_scale=scales[:, cols], start=True, stop=True,
+                    )
+            act = scratch([P, P, 4], F32, "act", None)
+            nc.scalar.activation(act[:], a[:].rearrange("p d n -> p n d"), SILU)
+            other = scratch([P, P, 4], F32, "other", None)
+            nc.scalar.copy(other[:], b[:].rearrange("p d n -> p n d"))
+            return act, other
+
+        def multiply_aside(act, other, h):
+            nc.gpsimd.tensor_tensor(h, act[:], other[:], MULT)
+
         def hidden_tile(place=None):
             return scratch([P, UNIT, 4], BF16, "h", place)
 
-        def quantize_shared(c, h):
-            cols = slice(c * UNIT, (c + 1) * UNIT)
-            nc.vector.quantize_mx(
-                out=hidden_codes[:, cols].bitcast(FP8X4), scales=hidden_scales[:, cols], in_=h[:].rearrange("p c j -> p (c j)")
-            )
-
-        def shared_last(half, bank):
-            cols = slice(half * 2 * UNIT, (half + 1) * 2 * UNIT)
-            ys = psum.tile([P, 2 * UNIT], F32, name=f"ys{half}", offset=bank * BANK)[:]
+        def shared_last(hq, bank):
+            codes, scales = hq
+            ys = psum.tile([P, UNIT], F32, name=f"ys{bank}", offset=bank * BANK)[:]
             nc.tensor.matmul_mx(
                 out=ys, lhsT=w2[:, SHARED, :].bitcast(FP4X4), lhsT_scale=s2[:, SHARED, :],
-                rhs=hidden_codes[:, cols].bitcast(FP8X4), rhs_scale=hidden_scales[:, cols], start=True, stop=True,
+                rhs=codes[:].bitcast(FP8X4), rhs_scale=scales[:], start=True, stop=True,
             )
             return ys
+
+        def quantize_shared(h, place=None):
+            return quantize("s", h[:].rearrange("p c j -> p (c j)"), place)
 
         def routed_tile(xq, e, pair, place=None):
             codes, scales = xq
@@ -272,7 +287,7 @@ def tile_moe_shr_glu_silu_kernel(tc, xT, w1_words, w1_scales, w3_words, w3_scale
             load_scale_rows(s3, w3_scales, 0, E, r)
         cast_pairs(1, nc.scalar.copy)
         xq1 = quantize("x", flat)
-        hs = [hidden_tile(H0_AT), hidden_tile(), hidden_tile(), hidden_tile()]
+        hs = [hidden_tile(H0_AT), hidden_tile()]
         cast_pairs(2, nc.vector.tensor_copy)
         cast_pairs(3, nc.vector.tensor_copy)
 
@@ -282,36 +297,37 @@ def tile_moe_shr_glu_silu_kernel(tc, xT, w1_words, w1_scales, w3_words, w3_scale
         shared_tile(xq0, hs[0], 1, 1, SILU_0B_AT)
         nc.sync.dma_start(out=gates[:], in_=gate)
         r0 = quantize("x", weave(p0))
-        quantize_shared(0, hs[0])
+        sq0 = quantize_shared(hs[0])
         shared_tile(xq1, hs[1], 0, 0, SILU_1A_AT)
         shared_tile(xq1, hs[1], 1, 1)
         p1 = gather(1, SILU_1A_AT)
-        quantize_shared(1, hs[1])
+        sq1 = quantize_shared(hs[1])
         xq2 = quantize("x", weave(pairs[:, :, 2 * UNIT : 3 * UNIT], "before_last_gather"))
         r1 = quantize("x", weave(p1))
         p2 = gather(2, "before_last_gather")
-        shared_tile(xq2, hs[2], 0, 2)
-        shared_tile(xq2, hs[2], 1, 3)
-        r2 = quantize("x", weave(p2))
-        quantize_shared(2, hs[2])
+        aside = shared_tile_aside(xq2, 0, 2)
+        r2 = quantize("x", weave(p2, "before_aside"))
+        h2 = hidden_tile("before_aside")
+        multiply_aside(*aside, h2[:, 0:P, :])
+        shared_tile(xq2, h2, 1, 3)
 
         rows0 = [routed_tile(r0, 0, 0), routed_tile(r0, 1, 1, "before_last_unit")]
-        rows1 = [routed_tile(r1, 2, 2), routed_tile(r1, 3, 0)]
+        rows1 = [routed_tile(r1, 2, 2, "before_sq2"), routed_tile(r1, 3, 0)]
         xq3 = quantize("x", weave(pairs[:, :, 3 * UNIT : 4 * UNIT], "before_last_unit"))
+        sq2 = quantize_shared(h2, "before_sq2")
         hq0 = quantize("h", turn(rows0))
         rows2 = [routed_tile(r2, 4, 1), routed_tile(r2, 5, 2, "before_scatter0")]
         hq1 = quantize("h", turn(rows1))
         y0 = routed_last(0, hq0, "before_scatter0")
-        shared_tile(xq3, hs[3], 0, 0, "before_scatter1")
+        h3 = hidden_tile()
+        shared_tile(xq3, h3, 0, 0, "before_scatter1")
         scatter(0, y0)
         hq2 = quantize("h", turn(rows2))
         y1 = routed_last(1, hq1, "before_scatter1")
-        shared_tile(xq3, hs[3], 1, 1)
+        shared_tile(xq3, h3, 1, 1)
         scatter(1, y1)
-        quantize_shared(3, hs[3])
+        sq3 = quantize_shared(h3)
         scatter(2, routed_last(2, hq2))
 
-        finish(shared_last(0, TURN_BANK), 0)
-        late = shared_last(1, 2 * 2)
-        finish(late[:, 0:UNIT], 2 * UNIT)
-        finish(late[:, UNIT : 2 * UNIT], 3 * UNIT)
+        for c, (sq, bank) in enumerate(((sq0, TURN_BANK), (sq1, 4), (sq2, 5), (sq3, 0))):
+            finish(shared_last(sq, bank), c * UNIT)

@@ -25,21 +25,20 @@ TURN_BANK, ROUTED_BANK = 6, 7
 WORK_BUFS = 7
 FLOPS = 2 * (E * C + T) * (2 * K * H + H * N)
 
-X_BYTES = 4 * UNIT * 4
+HALF = T // 2
+X_BYTES = 2 * HALF * 4
 BUFFER = 2048
 EDGE = 64
-W1_AT = 0
-X0_AT = E * 2 * H - X_BYTES
-X1_AT = X0_AT + X_BYTES
-SHARED_W1_AT = X1_AT + X_BYTES
-X2_AT = SHARED_W1_AT + 2 * H
-H0_AT = X2_AT + X_BYTES + EDGE
-X3_AT = H0_AT + BUFFER - EDGE
-SILU_1A_AT = X3_AT + EDGE
-SILU_0B_AT = SILU_1A_AT + BUFFER
-SILU_0A_AT = 12 * BUFFER
+X_AT = (0, X_BYTES, 2 * X_BYTES, 3 * X_BYTES)
+ZEROS = 256
+S2_AT = 4 * X_BYTES
+STAGED_AT = S2_AT + (E + 1) * N - EDGE
+PICKED_AT = STAGED_AT + H // 2
+SILU_0B_AT = PICKED_AT + BUFFER
+SILU_0A_AT = SILU_0B_AT + 3 * BUFFER
 W2_AT = SILU_0A_AT - BUFFER // 2
-ZEROS = (2 * H + EDGE) // 4
+RUNS_AT = SILU_0A_AT + 2 * BUFFER
+SPLIT = 336
 
 
 def tile_moe_shr_glu_silu_kernel(tc, xT, w1_words, w1_scales, w3_words, w3_scales, w2_words, w2_scales, gate, offs, out):
@@ -52,33 +51,28 @@ def tile_moe_shr_glu_silu_kernel(tc, xT, w1_words, w1_scales, w3_words, w3_scale
 
         offsets = keep.tile([P, E * C // 16], U16, name="offsets")
         pairs = keep.tile([P, 2, T], U32, name="pairs", align_bytes=64)
+        w1 = keep.tile([P, E, 2 * H], U8, name="w1", align_bytes=64)
         w3 = keep.tile([P, E, 2 * H], U8, name="w3", align_bytes=64)
+        shared_w = [keep.tile([P, 2 * H], U8, name=f"shared_w{m}", align_bytes=64) for m in range(2)]
         shared_s = [keep.tile([P, H], U8, name=f"shared_s{m}", align_bytes=64) for m in range(2)]
-        planes = keep.tile([P, 2 * E * H + (E + 1) * N], U8, name="planes", align_bytes=64)
+        planes = keep.tile([P, 2 * E * H], U8, name="planes", align_bytes=64)
         s1 = planes[:, 0 : E * H].rearrange("p (e n) -> p e n", e=E)
         s3 = planes[:, E * H : 2 * E * H].rearrange("p (e n) -> p e n", e=E)
-        s2 = planes[:, 2 * E * H :].rearrange("p (e n) -> p e n", e=E + 1)
-        staged = [planes[:, 2 * E * H : 2 * E * H + H], planes[:, E * H - H // 2 : E * H + H // 2]]
         scattered = keep.tile([P, T], F32, name="scattered")
         result = keep.tile([P, T], F32, name="result")
         ident = keep.tile([P, P], F32, name="ident")
 
-        zeros = reuse.tile([P, ZEROS], F32, name="zeros", offset=SHARED_W1_AT - EDGE // 2)
-        shared_w = [
-            reuse.tile([P, 2 * H], U8, name="shared_w1", offset=SHARED_W1_AT, align_bytes=64),
-            keep.tile([P, 2 * H], U8, name="shared_w3", align_bytes=64),
-        ]
-        first1 = reuse.tile([P, 1, 2 * H], U8, name="first1", offset=X3_AT, align_bytes=64)
-        raw = [
-            reuse.tile([P, 4, UNIT], F32, name=f"raw{c}", offset=at, align_bytes=64)
-            for c, at in enumerate((X0_AT, X1_AT, X2_AT, X3_AT))
-        ]
-        w1 = reuse.tile([P, E, 2 * H], U8, name="w1", offset=W1_AT, align_bytes=64)
+        zeros = reuse.tile([P, 3 * X_BYTES // 4], F32, name="zeros", offset=X_AT[1])
+        staged3 = reuse.tile([P, H], U8, name="staged3", offset=STAGED_AT, align_bytes=64)
+        s2 = reuse.tile([P, E + 1, N], U8, name="s2", offset=S2_AT, align_bytes=64)[:]
+        staged = [planes[:, E * H - H // 2 : E * H + H // 2], staged3[:]]
+        raw = [reuse.tile([P, 2, HALF], F32, name=f"raw{piece}", offset=X_AT[piece], align_bytes=64) for piece in range(4)]
         w2 = reuse.tile([P, E + 1, 2 * N], U8, name="w2", offset=W2_AT, align_bytes=64)
         gates = reuse.tile([P, E * C], F32, name="gates", offset=SILU_0B_AT, align_bytes=64)
 
-        def load_x(c):
-            nc.sync.dma_start(out=raw[c][:], in_=xT.rearrange("(p j) t -> p j t", j=4)[:, :, c * UNIT : (c + 1) * UNIT])
+        def load_x(piece):
+            rows = xT.rearrange("(p h e) t -> h p e t", h=2, e=2)[piece // 2]
+            nc.sync.dma_start(out=raw[piece][:], in_=rows[:, :, piece % 2 * HALF : (piece % 2 + 1) * HALF])
 
         def load_words(tile, words, a, b):
             nc.sync.dma_start(out=tile.bitcast(I32), in_=words[a:b, 0].bitcast(I32).rearrange("e p n -> p e n"))
@@ -93,21 +87,21 @@ def tile_moe_shr_glu_silu_kernel(tc, xT, w1_words, w1_scales, w3_words, w3_scale
 
         nc.vector.memset(staged[0].bitcast(I32), 0)
         nc.vector.memset(staged[1].bitcast(I32), 0)
-        nc.vector.memset(zeros[:], 0.0)
-        nc.scalar.activation(scattered[:, 0:ZEROS], zeros[:], SILU, bias=staged[1][:, 0:4].bitcast(F32))
+        nc.vector.memset(zeros[:, 0:ZEROS], 0.0)
+        nc.scalar.activation(scattered[:, 0:ZEROS], zeros[:, 0:ZEROS], SILU, bias=staged[1][:, 0:4].bitcast(F32))
         nc.vector.memset(planes[:, E * H + H // 2 : 2 * E * H].bitcast(I32), 0)
-        nc.vector.memset(planes[:, 2 * E * H + H :].bitcast(I32), 0)
         nc.vector.memset(planes[:, 0 : E * H - H // 2].bitcast(I32), 0)
         nc.vector.memset(scattered[:, ZEROS:], 0.0)
 
         nc.sync.dma_start(offsets[:], offs)
-        load_words(first1[:], w1_words, SHARED, SHARED + 1)
-        load_words(w3[:, 0:1, :], w3_words, SHARED, SHARED + 1)
         load_x(0)
+        load_words(w1[:, 0:1, :], w1_words, SHARED, SHARED + 1)
+        load_words(w3[:, 0:1, :], w3_words, SHARED, SHARED + 1)
         load_scales(staged[0].rearrange("p (e n) -> p e n", e=1), w1_scales, SHARED, SHARED + 1)
         load_x(1)
-        load_x(2)
         load_scales(staged[1].rearrange("p (e n) -> p e n", e=1), w3_scales, SHARED, SHARED + 1)
+        load_x(2)
+        load_x(3)
         make_identity(nc, ident[:])
 
         def permute_words(matrix, words):
@@ -129,15 +123,11 @@ def tile_moe_shr_glu_silu_kernel(tc, xT, w1_words, w1_scales, w3_words, w3_scale
                 return reuse.tile(shape, dtype, name=f"{name}_{place}", offset=place, align_bytes=64)
             return reuse.tile(shape, dtype, name=name, tag=place, align_bytes=64)
 
-        def cast_quads(c):
-            quads = work.tile([P, UNIT, 4], BF16, name="quads", align_bytes=64)
-            nc.vector.tensor_copy(quads[:].rearrange("p (c i) j -> p c j i", i=4), raw[c][:].rearrange("p j (c i) -> p c j i", i=4))
-            return quads[:].rearrange("p c j -> p (c j)")
-
-        def cast_pairs(c, copy):
+        def cast_pairs(piece, copy, a=0, b=HALF):
+            at = piece % 2 * HALF
             copy(
-                pairs[:, :, c * UNIT : (c + 1) * UNIT].bitcast(BF16).rearrange("p h (t e) -> p h t e", e=2),
-                raw[c][:].rearrange("p (h e) t -> p h t e", e=2),
+                pairs[:, piece // 2, at + a : at + b].bitcast(BF16).rearrange("p (t e) -> p t e", e=2),
+                raw[piece][:, :, a:b].rearrange("p e t -> p t e"),
             )
 
         def weave(halves, place=None):
@@ -149,24 +139,20 @@ def tile_moe_shr_glu_silu_kernel(tc, xT, w1_words, w1_scales, w3_words, w3_scale
         def slots(u):
             return offsets[:, u * UNIT // 16 : (u + 1) * UNIT // 16]
 
-        def gather(u, place=None):
-            picked = scratch([P, 2, UNIT], U32, "picked", place)
-            for half in range(2):
-                nc.vector.tensor_copy(picked[:, half, :], pairs[:, half, :].indirect(slots(u)))
-            return picked[:]
+        def gather(picked, u, half):
+            nc.vector.tensor_copy(picked[u][:, half, :], pairs[:, half, :].indirect(slots(u)))
 
         def quantize(tag, flat, place=None):
-            codes = scratch([P, UNIT], U32, tag + "_codes", place)
-            scales = work.tile([P, UNIT], U8, name=tag + "_scales", align_bytes=64)
+            width = flat.shape[1] // 4
+            codes = scratch([P, width], U32, tag + "_codes", place)
+            scales = work.tile([P, width], U8, name=tag + "_scales", align_bytes=64)
             nc.vector.quantize_mx(out=codes[:].bitcast(FP8X4), scales=scales[:], in_=flat)
             return codes, scales
 
         def sum_banks(pair):
-            a = psum.tile([P, 4, P], F32, name=f"a{pair}", offset=2 * pair * BANK)
-            b = psum.tile([P, 4, P], F32, name=f"b{pair}", offset=(2 * pair + 1) * BANK)
-            return a, b
+            return [psum.tile([P, 4, P], F32, name=f"sums{bank}", offset=bank * BANK) for bank in pair]
 
-        def shared_tile(xq, h, t, pair, place=None):
+        def shared_sums(xq, t, pair, place=None):
             codes, scales = xq
             cols = slice(t * P, (t + 1) * P)
             a, b = sum_banks(pair)
@@ -179,44 +165,29 @@ def tile_moe_shr_glu_silu_kernel(tc, xT, w1_words, w1_scales, w3_words, w3_scale
                     )
             act = scratch([P, P, 4], F32, "act", place)
             nc.scalar.activation(act[:], a[:].rearrange("p d n -> p n d"), SILU)
-            nc.vector.tensor_tensor(h[:, cols, :], act[:], b[:].rearrange("p d n -> p n d"), MULT)
+            return act, b[:].rearrange("p d n -> p n d")
 
-        def shared_tile_aside(xq, t, pair):
-            codes, scales = xq
-            cols = slice(t * P, (t + 1) * P)
-            a, b = sum_banks(pair)
-            for matrix, acc in enumerate((a, b)):
-                for d in range(4):
-                    nc.tensor.matmul_mx(
-                        out=acc[:, d, :], lhsT=shared_w[matrix][:, 2 * d * P : 2 * (d + 1) * P].bitcast(FP4X4),
-                        lhsT_scale=shared_s[matrix][:, d * P : (d + 1) * P],
-                        rhs=codes[:, cols].bitcast(FP8X4), rhs_scale=scales[:, cols], start=True, stop=True,
-                    )
-            act = scratch([P, P, 4], F32, "act", None)
-            nc.scalar.activation(act[:], a[:].rearrange("p d n -> p n d"), SILU)
-            other = scratch([P, P, 4], F32, "other", None)
-            nc.scalar.copy(other[:], b[:].rearrange("p d n -> p n d"))
-            return act, other
-
-        def multiply_aside(act, other, h):
-            nc.gpsimd.tensor_tensor(h, act[:], other[:], MULT)
+        def shared_tile(xq, h, t, pair, place=None):
+            act, b = shared_sums(xq, t, pair, place)
+            nc.vector.tensor_tensor(h[:, t * P : (t + 1) * P, :], act[:], b, MULT)
 
         def hidden_tile(place=None):
             return scratch([P, UNIT, 4], BF16, "h", place)
 
-        def shared_last(hq, bank):
-            codes, scales = hq
+        def shared_last(parts, bank):
             ys = psum.tile([P, UNIT], F32, name=f"ys{bank}", offset=bank * BANK)[:]
-            nc.tensor.matmul_mx(
-                out=ys, lhsT=w2[:, SHARED, :].bitcast(FP4X4), lhsT_scale=s2[:, SHARED, :],
-                rhs=codes[:].bitcast(FP8X4), rhs_scale=scales[:], start=True, stop=True,
-            )
+            width = UNIT // len(parts)
+            for j, (codes, scales) in enumerate(parts):
+                nc.tensor.matmul_mx(
+                    out=ys[:, j * width : (j + 1) * width], lhsT=w2[:, SHARED, :].bitcast(FP4X4), lhsT_scale=s2[:, SHARED, :],
+                    rhs=codes[:].bitcast(FP8X4), rhs_scale=scales[:], start=True, stop=True,
+                )
             return ys
 
         def quantize_shared(h, place=None):
             return quantize("s", h[:].rearrange("p c j -> p (c j)"), place)
 
-        def routed_tile(xq, e, pair, place=None):
+        def routed_tile(xq, e, rows, pair, place=None):
             codes, scales = xq
             cols = slice(e % TILES * P, (e % TILES + 1) * P)
             a, b = (acc[:].rearrange("p d n -> p (d n)") for acc in sum_banks(pair))
@@ -228,29 +199,34 @@ def tile_moe_shr_glu_silu_kernel(tc, xT, w1_words, w1_scales, w3_words, w3_scale
             act = scratch([P, P, 4], F32, "act", place)
             act = act[:].rearrange("p n d -> p (n d)").rearrange("p (u m v) -> p u m v", u=2, v=2)
             nc.scalar.activation(act, a.rearrange("p (m u v) -> p u m v", u=2, v=2), SILU)
-            row = work.tile([P, H], BF16, name="row")
             nc.vector.tensor_tensor(
-                row[:].rearrange("p (u m v) -> p u m v", u=2, v=2), act,
+                rows[:, e % TILES, :].rearrange("p (u m v) -> p u m v", u=2, v=2), act,
                 b.rearrange("p (m u v) -> p u m v", u=2, v=2), MULT,
             )
-            return row
 
-        def turn(rows):
-            back = psum.tile([P, TILES, 2, P], F32, name="back", offset=TURN_BANK * BANK)
+        def run_places(run):
+            at = RUNS_AT + 3 * run * BUFFER
+            return at, at + BUFFER - EDGE, at + 2 * (BUFFER - EDGE)
+
+        def rows_tile(place):
+            return scratch([P, TILES, H], BF16, "rows", place)
+
+        def turn(rows, bank, place=None):
+            back = psum.tile([P, TILES, 2, P], F32, name=f"back{bank}", offset=bank * BANK)
             for t in range(TILES):
-                words = rows[t][:].bitcast(F32)
+                words = rows[:, t, :].bitcast(F32)
                 for u in range(2):
                     nc.tensor.transpose(back[:, t, u, :], words[:, u * P : (u + 1) * P], ident[:])
-            flat = hidden_tile()[:].rearrange("p c j -> p (c j)")
+            flat = hidden_tile(place)[:].rearrange("p c j -> p (c j)")
             nc.scalar.copy(
                 flat.bitcast(F32).rearrange("p (t r u) -> p t r u", t=TILES, u=2),
                 back[:].rearrange("p t u r -> p t r u"),
             )
             return flat
 
-        def routed_last(unit, hq, place=None):
+        def routed_last(unit, hq, bank, place=None):
             codes, scales = hq
-            y = psum.tile([P, UNIT], F32, name="y", offset=ROUTED_BANK * BANK)
+            y = psum.tile([P, UNIT], F32, name=f"y{bank}", offset=bank * BANK)
             for t in range(TILES):
                 e = unit * TILES + t
                 cols = slice(t * P, (t + 1) * P)
@@ -270,64 +246,68 @@ def tile_moe_shr_glu_silu_kernel(tc, xT, w1_words, w1_scales, w3_words, w3_scale
             nc.vector.tensor_tensor(result[:, cols], ys, scattered[:, cols], ADD)
             nc.sync.dma_start(out=out[:, cols], in_=result[:, cols])
 
-        permute_words(0, first1)
-        load_x(3)
+        cast_pairs(0, nc.scalar.copy)
+        permute_words(0, w1)
+        load_words(w1[:], w1_words, 0, E)
         permute_words(1, w3)
         load_words(w3[:], w3_words, 0, E)
-        flat = cast_quads(0)
         permute_scales(0)
-        cast_pairs(0, nc.scalar.copy)
-        load_scales(s2, w2_scales, 0, E + 1)
-        load_words(w1[:], w1_words, 0, E)
-        xq0 = quantize("x", flat)
-        flat = cast_quads(1)
-        permute_scales(1)
         for r in range(4):
             load_scale_rows(s1, w1_scales, 0, E, r)
             load_scale_rows(s3, w3_scales, 0, E, r)
-        cast_pairs(1, nc.scalar.copy)
-        xq1 = quantize("x", flat)
-        hs = [hidden_tile(H0_AT), hidden_tile()]
-        cast_pairs(2, nc.vector.tensor_copy)
+        cast_pairs(1, nc.vector.tensor_copy, 0, SPLIT)
+        cast_pairs(1, nc.scalar.copy, SPLIT, HALF)
+        permute_scales(1)
+        nc.vector.memset(s2.rearrange("p e n -> p (e n)").bitcast(I32), 0)
+        load_scales(s2, w2_scales, 0, E + 1)
+        picked = [scratch([P, 2, UNIT], U32, "picked", place) for place in (None, None, PICKED_AT)]
+        for u in range(3):
+            gather(picked, u, 0)
+        cast_pairs(2, nc.scalar.copy, 0, UNIT)
+        flat0 = weave(pairs[:, :, 0:UNIT])
+        cast_pairs(2, nc.scalar.copy, UNIT, HALF)
         cast_pairs(3, nc.vector.tensor_copy)
-
-        p0 = gather(0)
-        shared_tile(xq0, hs[0], 0, 0, SILU_0A_AT)
+        xq0 = quantize("x", flat0)
+        flat1 = weave(pairs[:, :, UNIT : 2 * UNIT])
+        for u in range(3):
+            gather(picked, u, 1)
+        xq1 = quantize("x", flat1)
+        h0, h1, h2, h3 = (hidden_tile() for c in range(4))
+        shared_tile(xq0, h0, 0, (0, 1), SILU_0A_AT)
         load_words(w2[:], w2_words, 0, E + 1)
-        shared_tile(xq0, hs[0], 1, 1, SILU_0B_AT)
+        r0 = quantize("x", weave(picked[0][:]))
+        shared_tile(xq0, h0, 1, (2, 3), SILU_0B_AT)
         nc.sync.dma_start(out=gates[:], in_=gate)
-        r0 = quantize("x", weave(p0))
-        sq0 = quantize_shared(hs[0])
-        shared_tile(xq1, hs[1], 0, 0, SILU_1A_AT)
-        shared_tile(xq1, hs[1], 1, 1)
-        p1 = gather(1, SILU_1A_AT)
-        sq1 = quantize_shared(hs[1])
-        xq2 = quantize("x", weave(pairs[:, :, 2 * UNIT : 3 * UNIT], "before_last_gather"))
-        r1 = quantize("x", weave(p1))
-        p2 = gather(2, "before_last_gather")
-        aside = shared_tile_aside(xq2, 0, 2)
-        r2 = quantize("x", weave(p2, "before_aside"))
-        h2 = hidden_tile("before_aside")
-        multiply_aside(*aside, h2[:, 0:P, :])
-        shared_tile(xq2, h2, 1, 3)
+        xq2 = quantize("x", weave(pairs[:, :, 2 * UNIT : 3 * UNIT]))
+        shared_tile(xq1, h1, 0, (0, 1))
+        r1 = quantize("x", weave(picked[1][:]))
+        shared_tile(xq1, h1, 1, (2, 3))
+        sq0 = quantize_shared(h0)
+        shared_tile(xq2, h2, 0, (4, 5))
+        r2 = quantize("x", weave(picked[2][:]))
+        shared_tile(xq2, h2, 1, (6, 7))
+        sq1 = quantize_shared(h1)
 
-        rows0 = [routed_tile(r0, 0, 0), routed_tile(r0, 1, 1, "before_last_unit")]
-        rows1 = [routed_tile(r1, 2, 2, "before_sq2"), routed_tile(r1, 3, 0)]
+        rows0, rows1, rows2 = (rows_tile(None) for u in range(3))
+        routed_tile(r0, 0, rows0, (0, 1))
+        routed_tile(r0, 1, rows0, (2, 3), "before_last_unit")
+        sq2 = quantize_shared(h2)
+        routed_tile(r1, 2, rows1, (4, 5))
+        routed_tile(r1, 3, rows1, (0, 1))
         xq3 = quantize("x", weave(pairs[:, :, 3 * UNIT : 4 * UNIT], "before_last_unit"))
-        sq2 = quantize_shared(h2, "before_sq2")
-        hq0 = quantize("h", turn(rows0))
-        rows2 = [routed_tile(r2, 4, 1), routed_tile(r2, 5, 2, "before_scatter0")]
-        hq1 = quantize("h", turn(rows1))
-        y0 = routed_last(0, hq0, "before_scatter0")
-        h3 = hidden_tile()
-        shared_tile(xq3, h3, 0, 0, "before_scatter1")
+        hq0 = quantize("h", turn(rows0, 6))
+        routed_tile(r2, 4, rows2, (2, 3))
+        routed_tile(r2, 5, rows2, (4, 5), "before_scatter0")
+        hq1 = quantize("h", turn(rows1, 6))
+        y0 = routed_last(0, hq0, 7, "before_scatter0")
+        shared_tile(xq3, h3, 0, (0, 1), "before_scatter1")
         scatter(0, y0)
-        hq2 = quantize("h", turn(rows2))
-        y1 = routed_last(1, hq1, "before_scatter1")
-        shared_tile(xq3, h3, 1, 1)
+        hq2 = quantize("h", turn(rows2, 6))
+        y1 = routed_last(1, hq1, 7, "before_scatter1")
+        shared_tile(xq3, h3, 1, (2, 3))
         scatter(1, y1)
         sq3 = quantize_shared(h3)
-        scatter(2, routed_last(2, hq2))
+        scatter(2, routed_last(2, hq2, 7))
 
-        for c, (sq, bank) in enumerate(((sq0, TURN_BANK), (sq1, 4), (sq2, 5), (sq3, 0))):
-            finish(shared_last(sq, bank), c * UNIT)
+        for c, (sq, bank) in enumerate(((sq0, 6), (sq1, 4), (sq2, 5), (sq3, 0))):
+            finish(shared_last([sq], bank), c * UNIT)

@@ -29,16 +29,19 @@ HALF = T // 2
 X_BYTES = 2 * HALF * 4
 BUFFER = 2048
 EDGE = 64
-X_AT = (0, X_BYTES, 2 * X_BYTES, 3 * X_BYTES)
+X_AT = (0, X_BYTES, 5 * X_BYTES // 2 + H, 3 * X_BYTES + H)
 ZEROS = 256
-S2_AT = 4 * X_BYTES
-STAGED_AT = S2_AT + (E + 1) * N - EDGE
-PICKED_AT = STAGED_AT + H // 2
-SILU_0B_AT = PICKED_AT + BUFFER
-SILU_0A_AT = SILU_0B_AT + 3 * BUFFER
-W2_AT = SILU_0A_AT - BUFFER // 2
-RUNS_AT = SILU_0A_AT + 2 * BUFFER
-SPLIT = 336
+S2_AT = 4 * X_BYTES + H
+STAGED_AT = S2_AT + (E + 1) * N
+PICKED_AT = STAGED_AT + H - EDGE
+SILU_0B_AT = X_AT[3]
+SILU_0A_AT = SILU_0B_AT + BUFFER
+W2_AT = SILU_0A_AT
+GATES_AT = SILU_0B_AT - BUFFER // 2
+STAGED3_AT = PICKED_AT + 2 * BUFFER + EDGE
+PICKED2_AT = STAGED3_AT + H - EDGE
+RUNS_AT = PICKED2_AT + BUFFER + EDGE
+SPLIT = 512
 
 
 def tile_moe_shr_glu_silu_kernel(tc, xT, w1_words, w1_scales, w3_words, w3_scales, w2_words, w2_scales, gate, offs, out):
@@ -62,17 +65,23 @@ def tile_moe_shr_glu_silu_kernel(tc, xT, w1_words, w1_scales, w3_words, w3_scale
         result = keep.tile([P, T], F32, name="result")
         ident = keep.tile([P, P], F32, name="ident")
 
-        zeros = reuse.tile([P, 3 * X_BYTES // 4], F32, name="zeros", offset=X_AT[1])
-        staged3 = reuse.tile([P, H], U8, name="staged3", offset=STAGED_AT, align_bytes=64)
+        zeros = reuse.tile([P, 3 * X_BYTES // 8], F32, name="zeros", offset=X_AT[2])
+        staged1 = reuse.tile([P, H], U8, name="staged1", offset=STAGED_AT, align_bytes=64)
+        staged3 = reuse.tile([P, H], U8, name="staged3", offset=STAGED3_AT, align_bytes=64)
+        picked01 = reuse.tile([P, 2, 2 * UNIT], U32, name="picked01", offset=PICKED_AT, align_bytes=64)
+        picked2 = reuse.tile([P, 2, UNIT], U32, name="picked2", offset=PICKED2_AT, align_bytes=64)
+        picked = [picked01[:, :, 0:UNIT], picked01[:, :, UNIT : 2 * UNIT], picked2[:]]
         s2 = reuse.tile([P, E + 1, N], U8, name="s2", offset=S2_AT, align_bytes=64)[:]
-        staged = [planes[:, E * H - H // 2 : E * H + H // 2], staged3[:]]
-        raw = [reuse.tile([P, 2, HALF], F32, name=f"raw{piece}", offset=X_AT[piece], align_bytes=64) for piece in range(4)]
+        staged = [staged1[:], staged3[:]]
+        border = planes[:, E * H - 2 * ZEROS : E * H + 2 * ZEROS]
+        pieces = ((0, 4, 0, UNIT), (0, 2, UNIT, T - UNIT), (2, 2, UNIT, UNIT), (2, 2, HALF, HALF))
+        raw = [reuse.tile([P, pieces[j][1], pieces[j][3]], F32, name=f"raw{j}", offset=X_AT[j], align_bytes=64) for j in range(4)]
         w2 = reuse.tile([P, E + 1, 2 * N], U8, name="w2", offset=W2_AT, align_bytes=64)
-        gates = reuse.tile([P, E * C], F32, name="gates", offset=SILU_0B_AT, align_bytes=64)
+        gates = reuse.tile([P, E * C], F32, name="gates", offset=GATES_AT, align_bytes=64)
 
         def load_x(piece):
-            rows = xT.rearrange("(p h e) t -> h p e t", h=2, e=2)[piece // 2]
-            nc.sync.dma_start(out=raw[piece][:], in_=rows[:, :, piece % 2 * HALF : (piece % 2 + 1) * HALF])
+            row, rows, at, tokens = pieces[piece]
+            nc.sync.dma_start(out=raw[piece][:], in_=xT.rearrange("(p j) t -> p j t", j=4)[:, row : row + rows, at : at + tokens])
 
         def load_words(tile, words, a, b):
             nc.sync.dma_start(out=tile.bitcast(I32), in_=words[a:b, 0].bitcast(I32).rearrange("e p n -> p e n"))
@@ -87,21 +96,23 @@ def tile_moe_shr_glu_silu_kernel(tc, xT, w1_words, w1_scales, w3_words, w3_scale
 
         nc.vector.memset(staged[0].bitcast(I32), 0)
         nc.vector.memset(staged[1].bitcast(I32), 0)
-        nc.vector.memset(zeros[:, 0:ZEROS], 0.0)
-        nc.scalar.activation(scattered[:, 0:ZEROS], zeros[:, 0:ZEROS], SILU, bias=staged[1][:, 0:4].bitcast(F32))
-        nc.vector.memset(planes[:, E * H + H // 2 : 2 * E * H].bitcast(I32), 0)
-        nc.vector.memset(planes[:, 0 : E * H - H // 2].bitcast(I32), 0)
+        nc.vector.memset(zeros[:, 0:1], 0.0)
+        nc.vector.memset(border.bitcast(I32), 0)
+        nc.scalar.activation(scattered[:, 0:ZEROS], border.bitcast(F32), SILU, bias=staged[1][:, 0:4].bitcast(F32), scale=zeros[:, 0:1])
+        nc.vector.memset(planes[:, E * H + 2 * ZEROS : 2 * E * H].bitcast(I32), 0)
+        nc.vector.memset(planes[:, 0 : E * H - 2 * ZEROS].bitcast(I32), 0)
         nc.vector.memset(scattered[:, ZEROS:], 0.0)
+        nc.vector.memset(s2.rearrange("p e n -> p (e n)").bitcast(I32), 0)
 
-        nc.sync.dma_start(offsets[:], offs)
-        load_x(0)
         load_words(w1[:, 0:1, :], w1_words, SHARED, SHARED + 1)
         load_words(w3[:, 0:1, :], w3_words, SHARED, SHARED + 1)
-        load_scales(staged[0].rearrange("p (e n) -> p e n", e=1), w1_scales, SHARED, SHARED + 1)
+        load_x(0)
         load_x(1)
-        load_scales(staged[1].rearrange("p (e n) -> p e n", e=1), w3_scales, SHARED, SHARED + 1)
+        nc.sync.dma_start(offsets[:], offs)
+        load_scales(staged[0].rearrange("p (e n) -> p e n", e=1), w1_scales, SHARED, SHARED + 1)
         load_x(2)
         load_x(3)
+        load_scales(staged[1].rearrange("p (e n) -> p e n", e=1), w3_scales, SHARED, SHARED + 1)
         make_identity(nc, ident[:])
 
         def permute_words(matrix, words):
@@ -123,11 +134,11 @@ def tile_moe_shr_glu_silu_kernel(tc, xT, w1_words, w1_scales, w3_words, w3_scale
                 return reuse.tile(shape, dtype, name=f"{name}_{place}", offset=place, align_bytes=64)
             return reuse.tile(shape, dtype, name=name, tag=place, align_bytes=64)
 
-        def cast_pairs(piece, copy, a=0, b=HALF):
-            at = piece % 2 * HALF
+        def cast_pairs(piece, half, copy, a, b):
+            row, rows, at, tokens = pieces[piece]
             copy(
-                pairs[:, piece // 2, at + a : at + b].bitcast(BF16).rearrange("p (t e) -> p t e", e=2),
-                raw[piece][:, :, a:b].rearrange("p e t -> p t e"),
+                pairs[:, half, at + a : at + b].bitcast(BF16).rearrange("p (t e) -> p t e", e=2),
+                raw[piece][:, 2 * half - row : 2 * half - row + 2, a:b].rearrange("p e t -> p t e"),
             )
 
         def weave(halves, place=None):
@@ -139,8 +150,8 @@ def tile_moe_shr_glu_silu_kernel(tc, xT, w1_words, w1_scales, w3_words, w3_scale
         def slots(u):
             return offsets[:, u * UNIT // 16 : (u + 1) * UNIT // 16]
 
-        def gather(picked, u, half):
-            nc.vector.tensor_copy(picked[u][:, half, :], pairs[:, half, :].indirect(slots(u)))
+        def gather(into, a, b, half):
+            nc.vector.tensor_copy(into[:, half, :], pairs[:, half, :].indirect(offsets[:, a // 16 : b // 16]))
 
         def quantize(tag, flat, place=None):
             width = flat.shape[1] // 4
@@ -152,7 +163,7 @@ def tile_moe_shr_glu_silu_kernel(tc, xT, w1_words, w1_scales, w3_words, w3_scale
         def sum_banks(pair):
             return [psum.tile([P, 4, P], F32, name=f"sums{bank}", offset=bank * BANK) for bank in pair]
 
-        def shared_sums(xq, t, pair, place=None):
+        def shared_sums(xq, t, pair, place=None, bias=0.0):
             codes, scales = xq
             cols = slice(t * P, (t + 1) * P)
             a, b = sum_banks(pair)
@@ -164,11 +175,11 @@ def tile_moe_shr_glu_silu_kernel(tc, xT, w1_words, w1_scales, w3_words, w3_scale
                         rhs=codes[:, cols].bitcast(FP8X4), rhs_scale=scales[:, cols], start=True, stop=True,
                     )
             act = scratch([P, P, 4], F32, "act", place)
-            nc.scalar.activation(act[:], a[:].rearrange("p d n -> p n d"), SILU)
+            nc.scalar.activation(act[:], a[:].rearrange("p d n -> p n d"), SILU, bias=bias)
             return act, b[:].rearrange("p d n -> p n d")
 
-        def shared_tile(xq, h, t, pair, place=None):
-            act, b = shared_sums(xq, t, pair, place)
+        def shared_tile(xq, h, t, pair, place=None, bias=0.0):
+            act, b = shared_sums(xq, t, pair, place, bias)
             nc.vector.tensor_tensor(h[:, t * P : (t + 1) * P, :], act[:], b, MULT)
 
         def hidden_tile(place=None):
@@ -246,68 +257,65 @@ def tile_moe_shr_glu_silu_kernel(tc, xT, w1_words, w1_scales, w3_words, w3_scale
             nc.vector.tensor_tensor(result[:, cols], ys, scattered[:, cols], ADD)
             nc.sync.dma_start(out=out[:, cols], in_=result[:, cols])
 
-        cast_pairs(0, nc.scalar.copy)
+        cast_pairs(0, 1, nc.scalar.copy, 0, UNIT)
         permute_words(0, w1)
         load_words(w1[:], w1_words, 0, E)
         permute_words(1, w3)
         load_words(w3[:], w3_words, 0, E)
+        cast_pairs(0, 0, nc.vector.tensor_copy, 0, UNIT)
+        xq0 = quantize("x", weave(pairs[:, :, 0:UNIT]))
+        cast_pairs(1, 0, nc.vector.tensor_copy, 0, SPLIT)
+        cast_pairs(1, 0, nc.scalar.copy, SPLIT, T - UNIT)
         permute_scales(0)
         for r in range(4):
             load_scale_rows(s1, w1_scales, 0, E, r)
             load_scale_rows(s3, w3_scales, 0, E, r)
-        cast_pairs(1, nc.vector.tensor_copy, 0, SPLIT)
-        cast_pairs(1, nc.scalar.copy, SPLIT, HALF)
-        permute_scales(1)
-        nc.vector.memset(s2.rearrange("p e n -> p (e n)").bitcast(I32), 0)
-        load_scales(s2, w2_scales, 0, E + 1)
-        picked = [scratch([P, 2, UNIT], U32, "picked", place) for place in (None, None, PICKED_AT)]
-        for u in range(3):
-            gather(picked, u, 0)
-        cast_pairs(2, nc.scalar.copy, 0, UNIT)
-        flat0 = weave(pairs[:, :, 0:UNIT])
-        cast_pairs(2, nc.scalar.copy, UNIT, HALF)
-        cast_pairs(3, nc.vector.tensor_copy)
-        xq0 = quantize("x", flat0)
+        gather(picked01, 0, 2 * UNIT, 0)
+        cast_pairs(2, 1, nc.scalar.copy, 0, UNIT)
         flat1 = weave(pairs[:, :, UNIT : 2 * UNIT])
-        for u in range(3):
-            gather(picked, u, 1)
+        cast_pairs(3, 1, nc.scalar.copy, 0, HALF)
+        permute_scales(1)
+        gather(picked2, 2 * UNIT, 3 * UNIT, 0)
         xq1 = quantize("x", flat1)
+        gather(picked01, 0, 2 * UNIT, 1)
+        gather(picked2, 2 * UNIT, 3 * UNIT, 1)
         h0, h1, h2, h3 = (hidden_tile() for c in range(4))
-        shared_tile(xq0, h0, 0, (0, 1), SILU_0A_AT)
+        shared_tile(xq0, h0, 0, (0, 1), SILU_0A_AT, s2[:, 0, 0:4].bitcast(F32))
+        load_scales(s2, w2_scales, 0, E + 1)
         load_words(w2[:], w2_words, 0, E + 1)
-        r0 = quantize("x", weave(picked[0][:]))
+        r0 = quantize("x", weave(picked[0]))
         shared_tile(xq0, h0, 1, (2, 3), SILU_0B_AT)
         nc.sync.dma_start(out=gates[:], in_=gate)
         xq2 = quantize("x", weave(pairs[:, :, 2 * UNIT : 3 * UNIT]))
-        shared_tile(xq1, h1, 0, (0, 1))
-        r1 = quantize("x", weave(picked[1][:]))
-        shared_tile(xq1, h1, 1, (2, 3))
+        shared_tile(xq1, h1, 0, (4, 5))
+        r1 = quantize("x", weave(picked[1]))
+        shared_tile(xq1, h1, 1, (6, 7))
         sq0 = quantize_shared(h0)
-        shared_tile(xq2, h2, 0, (4, 5))
-        r2 = quantize("x", weave(picked[2][:]))
-        shared_tile(xq2, h2, 1, (6, 7))
+        shared_tile(xq2, h2, 0, (0, 1))
+        r2 = quantize("x", weave(picked[2]))
+        shared_tile(xq2, h2, 1, (2, 3))
         sq1 = quantize_shared(h1)
 
         rows0, rows1, rows2 = (rows_tile(None) for u in range(3))
-        routed_tile(r0, 0, rows0, (0, 1))
-        routed_tile(r0, 1, rows0, (2, 3), "before_last_unit")
+        routed_tile(r0, 0, rows0, (4, 5))
+        routed_tile(r0, 1, rows0, (0, 1), "before_last_unit")
         sq2 = quantize_shared(h2)
-        routed_tile(r1, 2, rows1, (4, 5))
-        routed_tile(r1, 3, rows1, (0, 1))
+        routed_tile(r1, 2, rows1, (2, 3))
+        routed_tile(r1, 3, rows1, (4, 5))
         xq3 = quantize("x", weave(pairs[:, :, 3 * UNIT : 4 * UNIT], "before_last_unit"))
         hq0 = quantize("h", turn(rows0, 6))
-        routed_tile(r2, 4, rows2, (2, 3))
-        routed_tile(r2, 5, rows2, (4, 5), "before_scatter0")
+        routed_tile(r2, 4, rows2, (0, 1))
+        routed_tile(r2, 5, rows2, (2, 3), "before_scatter0")
         hq1 = quantize("h", turn(rows1, 6))
         y0 = routed_last(0, hq0, 7, "before_scatter0")
-        shared_tile(xq3, h3, 0, (0, 1), "before_scatter1")
+        shared_tile(xq3, h3, 0, (4, 5), "before_scatter1")
         scatter(0, y0)
         hq2 = quantize("h", turn(rows2, 6))
         y1 = routed_last(1, hq1, 7, "before_scatter1")
-        shared_tile(xq3, h3, 1, (2, 3))
+        shared_tile(xq3, h3, 1, (0, 1))
         scatter(1, y1)
-        sq3 = quantize_shared(h3)
         scatter(2, routed_last(2, hq2, 7))
+        sq3 = quantize_shared(h3)
 
-        for c, (sq, bank) in enumerate(((sq0, 6), (sq1, 4), (sq2, 5), (sq3, 0))):
+        for c, (sq, bank) in enumerate(((sq0, 6), (sq1, 2), (sq2, 3), (sq3, 4))):
             finish(shared_last([sq], bank), c * UNIT)

@@ -29,19 +29,20 @@ HALF = T // 2
 X_BYTES = 2 * HALF * 4
 BUFFER = 2048
 EDGE = 64
-X_AT = (0, X_BYTES, 5 * X_BYTES // 2 + H, 3 * X_BYTES + H)
+X_AT = (0, X_BYTES, 2 * X_BYTES, 3 * X_BYTES)
 ZEROS = 256
-S2_AT = 4 * X_BYTES + H
+LANDED3_AT = 4 * X_BYTES
+W3_AT = LANDED3_AT + 2 * H - EDGE
+S2_AT = W3_AT + E * 2 * H
 STAGED_AT = S2_AT + (E + 1) * N
 PICKED_AT = STAGED_AT + H - EDGE
 SILU_0B_AT = X_AT[3]
 SILU_0A_AT = SILU_0B_AT + BUFFER
 W2_AT = SILU_0A_AT
 GATES_AT = SILU_0B_AT - BUFFER // 2
-STAGED3_AT = PICKED_AT + 2 * BUFFER + EDGE
-PICKED2_AT = STAGED3_AT + H - EDGE
-RUNS_AT = PICKED2_AT + BUFFER + EDGE
-SPLIT = 512
+STAGED3_AT = PICKED_AT + 3 * BUFFER + EDGE
+RUNS_AT = STAGED3_AT + H
+SPLIT = 336
 
 
 def tile_moe_shr_glu_silu_kernel(tc, xT, w1_words, w1_scales, w3_words, w3_scales, w2_words, w2_scales, gate, offs, out):
@@ -55,7 +56,7 @@ def tile_moe_shr_glu_silu_kernel(tc, xT, w1_words, w1_scales, w3_words, w3_scale
         offsets = keep.tile([P, E * C // 16], U16, name="offsets")
         pairs = keep.tile([P, 2, T], U32, name="pairs", align_bytes=64)
         w1 = keep.tile([P, E, 2 * H], U8, name="w1", align_bytes=64)
-        w3 = keep.tile([P, E, 2 * H], U8, name="w3", align_bytes=64)
+        w3 = reuse.tile([P, E, 2 * H], U8, name="w3", offset=W3_AT, align_bytes=64)
         shared_w = [keep.tile([P, 2 * H], U8, name=f"shared_w{m}", align_bytes=64) for m in range(2)]
         shared_s = [keep.tile([P, H], U8, name=f"shared_s{m}", align_bytes=64) for m in range(2)]
         planes = keep.tile([P, 2 * E * H], U8, name="planes", align_bytes=64)
@@ -65,16 +66,17 @@ def tile_moe_shr_glu_silu_kernel(tc, xT, w1_words, w1_scales, w3_words, w3_scale
         result = keep.tile([P, T], F32, name="result")
         ident = keep.tile([P, P], F32, name="ident")
 
-        zeros = reuse.tile([P, 3 * X_BYTES // 8], F32, name="zeros", offset=X_AT[2])
+        zeros = reuse.tile([P, (2 * X_BYTES + EDGE) // 4], F32, name="zeros", offset=X_AT[2])
+        first_zeros = reuse.tile([P, H], U8, name="first_zeros", offset=X_AT[1], align_bytes=64)
+        landed3 = reuse.tile([P, 1, 2 * H], U8, name="landed3", offset=LANDED3_AT, align_bytes=64)
         staged1 = reuse.tile([P, H], U8, name="staged1", offset=STAGED_AT, align_bytes=64)
         staged3 = reuse.tile([P, H], U8, name="staged3", offset=STAGED3_AT, align_bytes=64)
-        picked01 = reuse.tile([P, 2, 2 * UNIT], U32, name="picked01", offset=PICKED_AT, align_bytes=64)
-        picked2 = reuse.tile([P, 2, UNIT], U32, name="picked2", offset=PICKED2_AT, align_bytes=64)
-        picked = [picked01[:, :, 0:UNIT], picked01[:, :, UNIT : 2 * UNIT], picked2[:]]
+        picked_all = reuse.tile([P, 2, E * C], U32, name="picked_all", offset=PICKED_AT, align_bytes=64)
+        picked = [picked_all[:, :, u * UNIT : (u + 1) * UNIT] for u in range(3)]
         s2 = reuse.tile([P, E + 1, N], U8, name="s2", offset=S2_AT, align_bytes=64)[:]
         staged = [staged1[:], staged3[:]]
         border = planes[:, E * H - 2 * ZEROS : E * H + 2 * ZEROS]
-        pieces = ((0, 4, 0, UNIT), (0, 2, UNIT, T - UNIT), (2, 2, UNIT, UNIT), (2, 2, HALF, HALF))
+        pieces = ((0, 2, 0, HALF), (0, 2, HALF, HALF), (2, 2, 0, HALF), (2, 2, HALF, HALF))
         raw = [reuse.tile([P, pieces[j][1], pieces[j][3]], F32, name=f"raw{j}", offset=X_AT[j], align_bytes=64) for j in range(4)]
         w2 = reuse.tile([P, E + 1, 2 * N], U8, name="w2", offset=W2_AT, align_bytes=64)
         gates = reuse.tile([P, E * C], F32, name="gates", offset=GATES_AT, align_bytes=64)
@@ -94,7 +96,8 @@ def tile_moe_shr_glu_silu_kernel(tc, xT, w1_words, w1_scales, w3_words, w3_scale
             for r in range(4):
                 load_scale_rows(plane, scales, a, b, r)
 
-        nc.vector.memset(staged[0].bitcast(I32), 0)
+        nc.vector.memset(first_zeros[:].bitcast(I32), 0)
+        nc.vector.tensor_copy(staged[0].bitcast(I32), first_zeros[:].bitcast(I32))
         nc.vector.memset(staged[1].bitcast(I32), 0)
         nc.vector.memset(zeros[:, 0:1], 0.0)
         nc.vector.memset(border.bitcast(I32), 0)
@@ -104,12 +107,12 @@ def tile_moe_shr_glu_silu_kernel(tc, xT, w1_words, w1_scales, w3_words, w3_scale
         nc.vector.memset(scattered[:, ZEROS:], 0.0)
         nc.vector.memset(s2.rearrange("p e n -> p (e n)").bitcast(I32), 0)
 
-        load_words(w1[:, 0:1, :], w1_words, SHARED, SHARED + 1)
-        load_words(w3[:, 0:1, :], w3_words, SHARED, SHARED + 1)
-        load_x(0)
-        load_x(1)
         nc.sync.dma_start(offsets[:], offs)
+        load_words(w1[:, 0:1, :], w1_words, SHARED, SHARED + 1)
+        load_x(0)
         load_scales(staged[0].rearrange("p (e n) -> p e n", e=1), w1_scales, SHARED, SHARED + 1)
+        load_x(1)
+        load_words(landed3[:], w3_words, SHARED, SHARED + 1)
         load_x(2)
         load_x(3)
         load_scales(staged[1].rearrange("p (e n) -> p e n", e=1), w3_scales, SHARED, SHARED + 1)
@@ -141,17 +144,17 @@ def tile_moe_shr_glu_silu_kernel(tc, xT, w1_words, w1_scales, w3_words, w3_scale
                 raw[piece][:, 2 * half - row : 2 * half - row + 2, a:b].rearrange("p e t -> p t e"),
             )
 
-        def weave(halves, place=None):
+        def weave(halves, place=None, copy=nc.scalar.copy):
             quads = scratch([P, UNIT, 4], BF16, "quads", place)
             flat = quads[:].rearrange("p c j -> p (c j)")
-            nc.scalar.copy(flat.bitcast(U32).rearrange("p (t h) -> p t h", h=2), halves.rearrange("p h t -> p t h"))
+            copy(flat.bitcast(U32).rearrange("p (t h) -> p t h", h=2), halves.rearrange("p h t -> p t h"))
             return flat
 
         def slots(u):
             return offsets[:, u * UNIT // 16 : (u + 1) * UNIT // 16]
 
-        def gather(into, a, b, half):
-            nc.vector.tensor_copy(into[:, half, :], pairs[:, half, :].indirect(offsets[:, a // 16 : b // 16]))
+        def gather(a, b, half):
+            nc.vector.tensor_copy(picked_all[:, half, a:b], pairs[:, half, :].indirect(offsets[:, a // 16 : b // 16]))
 
         def quantize(tag, flat, place=None):
             width = flat.shape[1] // 4
@@ -257,28 +260,31 @@ def tile_moe_shr_glu_silu_kernel(tc, xT, w1_words, w1_scales, w3_words, w3_scale
             nc.vector.tensor_tensor(result[:, cols], ys, scattered[:, cols], ADD)
             nc.sync.dma_start(out=out[:, cols], in_=result[:, cols])
 
-        cast_pairs(0, 1, nc.scalar.copy, 0, UNIT)
+        cast_pairs(0, 0, nc.scalar.copy, 0, HALF)
         permute_words(0, w1)
         load_words(w1[:], w1_words, 0, E)
-        permute_words(1, w3)
-        load_words(w3[:], w3_words, 0, E)
-        cast_pairs(0, 0, nc.vector.tensor_copy, 0, UNIT)
-        xq0 = quantize("x", weave(pairs[:, :, 0:UNIT]))
-        cast_pairs(1, 0, nc.vector.tensor_copy, 0, SPLIT)
-        cast_pairs(1, 0, nc.scalar.copy, SPLIT, T - UNIT)
         permute_scales(0)
+        cast_pairs(1, 0, nc.vector.tensor_copy, 0, SPLIT)
+        cast_pairs(1, 0, nc.scalar.copy, SPLIT, HALF)
         for r in range(4):
             load_scale_rows(s1, w1_scales, 0, E, r)
             load_scale_rows(s3, w3_scales, 0, E, r)
-        gather(picked01, 0, 2 * UNIT, 0)
+        gather(0, E * C, 0)
+        permute_words(1, landed3)
+        load_words(w3[:], w3_words, 0, E)
         cast_pairs(2, 1, nc.scalar.copy, 0, UNIT)
-        flat1 = weave(pairs[:, :, UNIT : 2 * UNIT])
-        cast_pairs(3, 1, nc.scalar.copy, 0, HALF)
+        flat0 = weave(pairs[:, :, 0:UNIT])
+        cast_pairs(2, 1, nc.scalar.copy, UNIT, HALF)
+        cast_pairs(3, 1, nc.vector.tensor_copy, 0, HALF)
+        xq0 = quantize("x", flat0)
         permute_scales(1)
-        gather(picked2, 2 * UNIT, 3 * UNIT, 0)
+        flat1 = weave(pairs[:, :, UNIT : 2 * UNIT])
+        gather(0, UNIT, 1)
+        gather(UNIT, E * C, 1)
         xq1 = quantize("x", flat1)
-        gather(picked01, 0, 2 * UNIT, 1)
-        gather(picked2, 2 * UNIT, 3 * UNIT, 1)
+        flat_r1 = weave(picked[1], None, nc.vector.tensor_copy)
+        xq2 = quantize("x", weave(pairs[:, :, 2 * UNIT : 3 * UNIT]))
+        r1 = quantize("x", flat_r1)
         h0, h1, h2, h3 = (hidden_tile() for c in range(4))
         shared_tile(xq0, h0, 0, (0, 1), SILU_0A_AT, s2[:, 0, 0:4].bitcast(F32))
         load_scales(s2, w2_scales, 0, E + 1)
@@ -286,11 +292,9 @@ def tile_moe_shr_glu_silu_kernel(tc, xT, w1_words, w1_scales, w3_words, w3_scale
         r0 = quantize("x", weave(picked[0]))
         shared_tile(xq0, h0, 1, (2, 3), SILU_0B_AT)
         nc.sync.dma_start(out=gates[:], in_=gate)
-        xq2 = quantize("x", weave(pairs[:, :, 2 * UNIT : 3 * UNIT]))
         shared_tile(xq1, h1, 0, (4, 5))
-        r1 = quantize("x", weave(picked[1]))
-        shared_tile(xq1, h1, 1, (6, 7))
         sq0 = quantize_shared(h0)
+        shared_tile(xq1, h1, 1, (6, 7))
         shared_tile(xq2, h2, 0, (0, 1))
         r2 = quantize("x", weave(picked[2]))
         shared_tile(xq2, h2, 1, (2, 3))

@@ -19,30 +19,32 @@ P = 128
 K, T, E, C, H, N = 512, 1024, 6, 128, 512, 128
 SHARED = E
 UNIT = 256
-TILES = UNIT // P
-BANK = 2048
-TURN_BANK, ROUTED_BANK = 6, 7
+PARTS = UNIT // P
+HALF = T // 2
+SPLIT = 336
+ZEROS = 256
 WORK_BUFS = 7
 FLOPS = 2 * (E * C + T) * (2 * K * H + H * N)
 
-HALF = T // 2
+BANK = 2048
+PAIRS = ((0, 1), (2, 3), (4, 5), (6, 7))
+TURN_BANK, ROUTED_BANK = PAIRS[3]
+RESULT_BANKS = (TURN_BANK, *PAIRS[1], PAIRS[2][0])
+
 X_BYTES = 2 * HALF * 4
 BUFFER = 2048
 EDGE = 64
 X_AT = (0, X_BYTES, 2 * X_BYTES, 3 * X_BYTES)
-ZEROS = 256
 LANDED3_AT = 4 * X_BYTES
 W3_AT = LANDED3_AT + 2 * H - EDGE
 S2_AT = W3_AT + E * 2 * H
-STAGED_AT = S2_AT + (E + 1) * N
-PICKED_AT = STAGED_AT + H - EDGE
-SILU_0B_AT = X_AT[3]
-SILU_0A_AT = SILU_0B_AT + BUFFER
-W2_AT = SILU_0A_AT
-GATES_AT = SILU_0B_AT - BUFFER // 2
-STAGED3_AT = PICKED_AT + 3 * BUFFER + EDGE
-RUNS_AT = STAGED3_AT + H
-SPLIT = 336
+STAGED1_AT = S2_AT + (E + 1) * N
+PICKED_AT = STAGED1_AT + H - EDGE
+STAGED3_AT = PICKED_AT + 2 * E * C * 4 + EDGE
+SECOND_SILU_AT = X_AT[3]
+FIRST_SILU_AT = SECOND_SILU_AT + BUFFER
+W2_AT = FIRST_SILU_AT
+GATES_AT = SECOND_SILU_AT - BUFFER // 2
 
 
 def tile_moe_shr_glu_silu_kernel(tc, xT, w1_words, w1_scales, w3_words, w3_scales, w2_words, w2_scales, gate, offs, out):
@@ -62,28 +64,27 @@ def tile_moe_shr_glu_silu_kernel(tc, xT, w1_words, w1_scales, w3_words, w3_scale
         planes = keep.tile([P, 2 * E * H], U8, name="planes", align_bytes=64)
         s1 = planes[:, 0 : E * H].rearrange("p (e n) -> p e n", e=E)
         s3 = planes[:, E * H : 2 * E * H].rearrange("p (e n) -> p e n", e=E)
+        border = planes[:, E * H - 2 * ZEROS : E * H + 2 * ZEROS]
         scattered = keep.tile([P, T], F32, name="scattered")
         result = keep.tile([P, T], F32, name="result")
         ident = keep.tile([P, P], F32, name="ident")
 
-        zeros = reuse.tile([P, (2 * X_BYTES + EDGE) // 4], F32, name="zeros", offset=X_AT[2])
+        late_zero = reuse.tile([P, (2 * X_BYTES + EDGE) // 4], F32, name="late_zero", offset=X_AT[2])
         first_zeros = reuse.tile([P, H], U8, name="first_zeros", offset=X_AT[1], align_bytes=64)
         landed3 = reuse.tile([P, 1, 2 * H], U8, name="landed3", offset=LANDED3_AT, align_bytes=64)
-        staged1 = reuse.tile([P, H], U8, name="staged1", offset=STAGED_AT, align_bytes=64)
-        staged3 = reuse.tile([P, H], U8, name="staged3", offset=STAGED3_AT, align_bytes=64)
-        picked_all = reuse.tile([P, 2, E * C], U32, name="picked_all", offset=PICKED_AT, align_bytes=64)
-        picked = [picked_all[:, :, u * UNIT : (u + 1) * UNIT] for u in range(3)]
+        staged = [
+            reuse.tile([P, H], U8, name=f"staged{m}", offset=at, align_bytes=64)[:]
+            for m, at in enumerate((STAGED1_AT, STAGED3_AT))
+        ]
+        picked = reuse.tile([P, 2, E * C], U32, name="picked", offset=PICKED_AT, align_bytes=64)
         s2 = reuse.tile([P, E + 1, N], U8, name="s2", offset=S2_AT, align_bytes=64)[:]
-        staged = [staged1[:], staged3[:]]
-        border = planes[:, E * H - 2 * ZEROS : E * H + 2 * ZEROS]
-        pieces = ((0, 2, 0, HALF), (0, 2, HALF, HALF), (2, 2, 0, HALF), (2, 2, HALF, HALF))
-        raw = [reuse.tile([P, pieces[j][1], pieces[j][3]], F32, name=f"raw{j}", offset=X_AT[j], align_bytes=64) for j in range(4)]
+        raw = [reuse.tile([P, 2, HALF], F32, name=f"raw{piece}", offset=X_AT[piece], align_bytes=64) for piece in range(4)]
         w2 = reuse.tile([P, E + 1, 2 * N], U8, name="w2", offset=W2_AT, align_bytes=64)
         gates = reuse.tile([P, E * C], F32, name="gates", offset=GATES_AT, align_bytes=64)
 
         def load_x(piece):
-            row, rows, at, tokens = pieces[piece]
-            nc.sync.dma_start(out=raw[piece][:], in_=xT.rearrange("(p j) t -> p j t", j=4)[:, row : row + rows, at : at + tokens])
+            row, at = piece // 2 * 2, piece % 2 * HALF
+            nc.sync.dma_start(out=raw[piece][:], in_=xT.rearrange("(p j) t -> p j t", j=4)[:, row : row + 2, at : at + HALF])
 
         def load_words(tile, words, a, b):
             nc.sync.dma_start(out=tile.bitcast(I32), in_=words[a:b, 0].bitcast(I32).rearrange("e p n -> p e n"))
@@ -99,9 +100,11 @@ def tile_moe_shr_glu_silu_kernel(tc, xT, w1_words, w1_scales, w3_words, w3_scale
         nc.vector.memset(first_zeros[:].bitcast(I32), 0)
         nc.vector.tensor_copy(staged[0].bitcast(I32), first_zeros[:].bitcast(I32))
         nc.vector.memset(staged[1].bitcast(I32), 0)
-        nc.vector.memset(zeros[:, 0:1], 0.0)
+        nc.vector.memset(late_zero[:, 0:1], 0.0)
         nc.vector.memset(border.bitcast(I32), 0)
-        nc.scalar.activation(scattered[:, 0:ZEROS], border.bitcast(F32), SILU, bias=staged[1][:, 0:4].bitcast(F32), scale=zeros[:, 0:1])
+        nc.scalar.activation(
+            scattered[:, 0:ZEROS], border.bitcast(F32), SILU, bias=staged[1][:, 0:4].bitcast(F32), scale=late_zero[:, 0:1]
+        )
         nc.vector.memset(planes[:, E * H + 2 * ZEROS : 2 * E * H].bitcast(I32), 0)
         nc.vector.memset(planes[:, 0 : E * H - 2 * ZEROS].bitcast(I32), 0)
         nc.vector.memset(scattered[:, ZEROS:], 0.0)
@@ -137,38 +140,38 @@ def tile_moe_shr_glu_silu_kernel(tc, xT, w1_words, w1_scales, w3_words, w3_scale
                 return reuse.tile(shape, dtype, name=f"{name}_{place}", offset=place, align_bytes=64)
             return reuse.tile(shape, dtype, name=name, tag=place, align_bytes=64)
 
-        def cast_pairs(piece, half, copy, a, b):
-            row, rows, at, tokens = pieces[piece]
+        def round_pairs(piece, copy, a, b):
+            at = piece % 2 * HALF
             copy(
-                pairs[:, half, at + a : at + b].bitcast(BF16).rearrange("p (t e) -> p t e", e=2),
-                raw[piece][:, 2 * half - row : 2 * half - row + 2, a:b].rearrange("p e t -> p t e"),
+                pairs[:, piece // 2, at + a : at + b].bitcast(BF16).rearrange("p (t e) -> p t e", e=2),
+                raw[piece][:, :, a:b].rearrange("p e t -> p t e"),
             )
 
-        def weave(halves, place=None, copy=nc.scalar.copy):
+        def weave(words, unit, place=None, copy=nc.scalar.copy):
             quads = scratch([P, UNIT, 4], BF16, "quads", place)
             flat = quads[:].rearrange("p c j -> p (c j)")
+            halves = words[:, :, unit * UNIT : (unit + 1) * UNIT]
             copy(flat.bitcast(U32).rearrange("p (t h) -> p t h", h=2), halves.rearrange("p h t -> p t h"))
             return flat
 
-        def slots(u):
-            return offsets[:, u * UNIT // 16 : (u + 1) * UNIT // 16]
+        def slots(a, b):
+            return offsets[:, a // 16 : b // 16]
 
         def gather(a, b, half):
-            nc.vector.tensor_copy(picked_all[:, half, a:b], pairs[:, half, :].indirect(offsets[:, a // 16 : b // 16]))
+            nc.vector.tensor_copy(picked[:, half, a:b], pairs[:, half, :].indirect(slots(a, b)))
 
-        def quantize(tag, flat, place=None):
-            width = flat.shape[1] // 4
-            codes = scratch([P, width], U32, tag + "_codes", place)
-            scales = work.tile([P, width], U8, name=tag + "_scales", align_bytes=64)
+        def quantize(tag, flat):
+            codes = work.tile([P, UNIT], U32, name=tag + "_codes", align_bytes=64)
+            scales = work.tile([P, UNIT], U8, name=tag + "_scales", align_bytes=64)
             nc.vector.quantize_mx(out=codes[:].bitcast(FP8X4), scales=scales[:], in_=flat)
             return codes, scales
 
         def sum_banks(pair):
-            return [psum.tile([P, 4, P], F32, name=f"sums{bank}", offset=bank * BANK) for bank in pair]
+            return [psum.tile([P, 4, P], F32, name=f"sums{bank}", offset=bank * BANK) for bank in PAIRS[pair]]
 
-        def shared_sums(xq, t, pair, place=None, bias=0.0):
+        def shared_part(xq, h, part, pair, place=None, bias=0.0):
             codes, scales = xq
-            cols = slice(t * P, (t + 1) * P)
+            cols = slice(part * P, (part + 1) * P)
             a, b = sum_banks(pair)
             for matrix, acc in enumerate((a, b)):
                 for d in range(4):
@@ -179,31 +182,17 @@ def tile_moe_shr_glu_silu_kernel(tc, xT, w1_words, w1_scales, w3_words, w3_scale
                     )
             act = scratch([P, P, 4], F32, "act", place)
             nc.scalar.activation(act[:], a[:].rearrange("p d n -> p n d"), SILU, bias=bias)
-            return act, b[:].rearrange("p d n -> p n d")
+            nc.vector.tensor_tensor(h[:, cols, :], act[:], b[:].rearrange("p d n -> p n d"), MULT)
 
-        def shared_tile(xq, h, t, pair, place=None, bias=0.0):
-            act, b = shared_sums(xq, t, pair, place, bias)
-            nc.vector.tensor_tensor(h[:, t * P : (t + 1) * P, :], act[:], b, MULT)
+        def hidden_tile():
+            return work.tile([P, UNIT, 4], BF16, name="h", align_bytes=64)
 
-        def hidden_tile(place=None):
-            return scratch([P, UNIT, 4], BF16, "h", place)
+        def quantize_shared(h):
+            return quantize("s", h[:].rearrange("p c j -> p (c j)"))
 
-        def shared_last(parts, bank):
-            ys = psum.tile([P, UNIT], F32, name=f"ys{bank}", offset=bank * BANK)[:]
-            width = UNIT // len(parts)
-            for j, (codes, scales) in enumerate(parts):
-                nc.tensor.matmul_mx(
-                    out=ys[:, j * width : (j + 1) * width], lhsT=w2[:, SHARED, :].bitcast(FP4X4), lhsT_scale=s2[:, SHARED, :],
-                    rhs=codes[:].bitcast(FP8X4), rhs_scale=scales[:], start=True, stop=True,
-                )
-            return ys
-
-        def quantize_shared(h, place=None):
-            return quantize("s", h[:].rearrange("p c j -> p (c j)"), place)
-
-        def routed_tile(xq, e, rows, pair, place=None):
+        def routed_part(xq, e, rows, pair, place=None):
             codes, scales = xq
-            cols = slice(e % TILES * P, (e % TILES + 1) * P)
+            cols = slice(e % PARTS * P, (e % PARTS + 1) * P)
             a, b = (acc[:].rearrange("p d n -> p (d n)") for acc in sum_banks(pair))
             for acc, w, s in ((a, w1, s1), (b, w3, s3)):
                 nc.tensor.matmul_mx(
@@ -214,36 +203,29 @@ def tile_moe_shr_glu_silu_kernel(tc, xT, w1_words, w1_scales, w3_words, w3_scale
             act = act[:].rearrange("p n d -> p (n d)").rearrange("p (u m v) -> p u m v", u=2, v=2)
             nc.scalar.activation(act, a.rearrange("p (m u v) -> p u m v", u=2, v=2), SILU)
             nc.vector.tensor_tensor(
-                rows[:, e % TILES, :].rearrange("p (u m v) -> p u m v", u=2, v=2), act,
+                rows[:, e % PARTS, :].rearrange("p (u m v) -> p u m v", u=2, v=2), act,
                 b.rearrange("p (m u v) -> p u m v", u=2, v=2), MULT,
             )
 
-        def run_places(run):
-            at = RUNS_AT + 3 * run * BUFFER
-            return at, at + BUFFER - EDGE, at + 2 * (BUFFER - EDGE)
-
-        def rows_tile(place):
-            return scratch([P, TILES, H], BF16, "rows", place)
-
-        def turn(rows, bank, place=None):
-            back = psum.tile([P, TILES, 2, P], F32, name=f"back{bank}", offset=bank * BANK)
-            for t in range(TILES):
-                words = rows[:, t, :].bitcast(F32)
+        def turn(rows):
+            back = psum.tile([P, PARTS, 2, P], F32, name="back", offset=TURN_BANK * BANK)
+            for part in range(PARTS):
+                words = rows[:, part, :].bitcast(F32)
                 for u in range(2):
-                    nc.tensor.transpose(back[:, t, u, :], words[:, u * P : (u + 1) * P], ident[:])
-            flat = hidden_tile(place)[:].rearrange("p c j -> p (c j)")
+                    nc.tensor.transpose(back[:, part, u, :], words[:, u * P : (u + 1) * P], ident[:])
+            flat = hidden_tile()[:].rearrange("p c j -> p (c j)")
             nc.scalar.copy(
-                flat.bitcast(F32).rearrange("p (t r u) -> p t r u", t=TILES, u=2),
+                flat.bitcast(F32).rearrange("p (t r u) -> p t r u", t=PARTS, u=2),
                 back[:].rearrange("p t u r -> p t r u"),
             )
             return flat
 
-        def routed_last(unit, hq, bank, place=None):
+        def routed_result(unit, hq, place=None):
             codes, scales = hq
-            y = psum.tile([P, UNIT], F32, name=f"y{bank}", offset=bank * BANK)
-            for t in range(TILES):
-                e = unit * TILES + t
-                cols = slice(t * P, (t + 1) * P)
+            y = psum.tile([P, UNIT], F32, name="y", offset=ROUTED_BANK * BANK)
+            for part in range(PARTS):
+                e = unit * PARTS + part
+                cols = slice(part * P, (part + 1) * P)
                 nc.tensor.matmul_mx(
                     out=y[:, cols], lhsT=w2[:, e, :].bitcast(FP4X4), lhsT_scale=s2[:, e, :],
                     rhs=codes[:, cols].bitcast(FP8X4), rhs_scale=scales[:, cols], start=True, stop=True,
@@ -253,73 +235,82 @@ def tile_moe_shr_glu_silu_kernel(tc, xT, w1_words, w1_scales, w3_words, w3_scale
             return ysb
 
         def scatter(unit, ysb):
-            nc.vector.tensor_tensor(scattered[:].indirect(slots(unit)), ysb[:], gates[:, unit * UNIT : (unit + 1) * UNIT], MULT)
+            a, b = unit * UNIT, (unit + 1) * UNIT
+            nc.vector.tensor_tensor(scattered[:].indirect(slots(a, b)), ysb[:], gates[:, a:b], MULT)
 
-        def finish(ys, at):
-            cols = slice(at, at + ys.shape[1])
-            nc.vector.tensor_tensor(result[:, cols], ys, scattered[:, cols], ADD)
+        def finish(unit, hq):
+            codes, scales = hq
+            cols = slice(unit * UNIT, (unit + 1) * UNIT)
+            ys = psum.tile([P, UNIT], F32, name=f"ys{unit}", offset=RESULT_BANKS[unit] * BANK)
+            nc.tensor.matmul_mx(
+                out=ys[:], lhsT=w2[:, SHARED, :].bitcast(FP4X4), lhsT_scale=s2[:, SHARED, :],
+                rhs=codes[:].bitcast(FP8X4), rhs_scale=scales[:], start=True, stop=True,
+            )
+            nc.vector.tensor_tensor(result[:, cols], ys[:], scattered[:, cols], ADD)
             nc.sync.dma_start(out=out[:, cols], in_=result[:, cols])
 
-        cast_pairs(0, 0, nc.scalar.copy, 0, HALF)
+        round_pairs(0, nc.scalar.copy, 0, HALF)
         permute_words(0, w1)
         load_words(w1[:], w1_words, 0, E)
         permute_scales(0)
-        cast_pairs(1, 0, nc.vector.tensor_copy, 0, SPLIT)
-        cast_pairs(1, 0, nc.scalar.copy, SPLIT, HALF)
+        round_pairs(1, nc.vector.tensor_copy, 0, SPLIT)
+        round_pairs(1, nc.scalar.copy, SPLIT, HALF)
         for r in range(4):
             load_scale_rows(s1, w1_scales, 0, E, r)
             load_scale_rows(s3, w3_scales, 0, E, r)
         gather(0, E * C, 0)
         permute_words(1, landed3)
         load_words(w3[:], w3_words, 0, E)
-        cast_pairs(2, 1, nc.scalar.copy, 0, UNIT)
-        flat0 = weave(pairs[:, :, 0:UNIT])
-        cast_pairs(2, 1, nc.scalar.copy, UNIT, HALF)
-        cast_pairs(3, 1, nc.vector.tensor_copy, 0, HALF)
+
+        round_pairs(2, nc.scalar.copy, 0, UNIT)
+        flat0 = weave(pairs, 0)
+        round_pairs(2, nc.scalar.copy, UNIT, HALF)
+        round_pairs(3, nc.vector.tensor_copy, 0, HALF)
         xq0 = quantize("x", flat0)
         permute_scales(1)
-        flat1 = weave(pairs[:, :, UNIT : 2 * UNIT])
+        flat1 = weave(pairs, 1)
         gather(0, UNIT, 1)
         gather(UNIT, E * C, 1)
         xq1 = quantize("x", flat1)
-        flat_r1 = weave(picked[1], None, nc.vector.tensor_copy)
-        xq2 = quantize("x", weave(pairs[:, :, 2 * UNIT : 3 * UNIT]))
+        flat_r1 = weave(picked, 1, None, nc.vector.tensor_copy)
+        xq2 = quantize("x", weave(pairs, 2))
         r1 = quantize("x", flat_r1)
-        h0, h1, h2, h3 = (hidden_tile() for c in range(4))
-        shared_tile(xq0, h0, 0, (0, 1), SILU_0A_AT, s2[:, 0, 0:4].bitcast(F32))
+
+        h0, h1, h2, h3 = (hidden_tile() for unit in range(4))
+        shared_part(xq0, h0, 0, 0, FIRST_SILU_AT, s2[:, 0, 0:4].bitcast(F32))
         load_scales(s2, w2_scales, 0, E + 1)
         load_words(w2[:], w2_words, 0, E + 1)
-        r0 = quantize("x", weave(picked[0]))
-        shared_tile(xq0, h0, 1, (2, 3), SILU_0B_AT)
+        r0 = quantize("x", weave(picked, 0))
+        shared_part(xq0, h0, 1, 1, SECOND_SILU_AT)
         nc.sync.dma_start(out=gates[:], in_=gate)
-        shared_tile(xq1, h1, 0, (4, 5))
+        shared_part(xq1, h1, 0, 2)
         sq0 = quantize_shared(h0)
-        shared_tile(xq1, h1, 1, (6, 7))
-        shared_tile(xq2, h2, 0, (0, 1))
-        r2 = quantize("x", weave(picked[2]))
-        shared_tile(xq2, h2, 1, (2, 3))
+        shared_part(xq1, h1, 1, 3)
+        shared_part(xq2, h2, 0, 0)
+        r2 = quantize("x", weave(picked, 2))
+        shared_part(xq2, h2, 1, 1)
         sq1 = quantize_shared(h1)
 
-        rows0, rows1, rows2 = (rows_tile(None) for u in range(3))
-        routed_tile(r0, 0, rows0, (4, 5))
-        routed_tile(r0, 1, rows0, (0, 1), "before_last_unit")
+        rows0, rows1, rows2 = (work.tile([P, PARTS, H], BF16, name="rows", align_bytes=64) for unit in range(3))
+        routed_part(r0, 0, rows0, 2)
+        routed_part(r0, 1, rows0, 0)
         sq2 = quantize_shared(h2)
-        routed_tile(r1, 2, rows1, (2, 3))
-        routed_tile(r1, 3, rows1, (4, 5))
-        xq3 = quantize("x", weave(pairs[:, :, 3 * UNIT : 4 * UNIT], "before_last_unit"))
-        hq0 = quantize("h", turn(rows0, 6))
-        routed_tile(r2, 4, rows2, (0, 1))
-        routed_tile(r2, 5, rows2, (2, 3), "before_scatter0")
-        hq1 = quantize("h", turn(rows1, 6))
-        y0 = routed_last(0, hq0, 7, "before_scatter0")
-        shared_tile(xq3, h3, 0, (4, 5), "before_scatter1")
+        routed_part(r1, 2, rows1, 1)
+        routed_part(r1, 3, rows1, 2, "before_last_unit")
+        hq0 = quantize("h", turn(rows0))
+        routed_part(r2, 4, rows2, 0)
+        routed_part(r2, 5, rows2, 1, "before_scatter0")
+        hq1 = quantize("h", turn(rows1))
+        y0 = routed_result(0, hq0, "before_scatter0")
+        xq3 = quantize("x", weave(pairs, 3, "before_last_unit"))
         scatter(0, y0)
-        hq2 = quantize("h", turn(rows2, 6))
-        y1 = routed_last(1, hq1, 7, "before_scatter1")
-        shared_tile(xq3, h3, 1, (0, 1))
+        shared_part(xq3, h3, 0, 2, "before_scatter1")
+        hq2 = quantize("h", turn(rows2))
+        y1 = routed_result(1, hq1, "before_scatter1")
+        shared_part(xq3, h3, 1, 0)
         scatter(1, y1)
-        scatter(2, routed_last(2, hq2, 7))
+        scatter(2, routed_result(2, hq2))
         sq3 = quantize_shared(h3)
 
-        for c, (sq, bank) in enumerate(((sq0, 6), (sq1, 2), (sq2, 3), (sq3, 4))):
-            finish(shared_last([sq], bank), c * UNIT)
+        for unit, sq in enumerate((sq0, sq1, sq2, sq3)):
+            finish(unit, sq)

@@ -41,6 +41,7 @@ S2_AT = W3_AT + E * 2 * H
 STAGED1_AT = S2_AT + (E + 1) * N
 PICKED_AT = STAGED1_AT + H - EDGE
 STAGED3_AT = PICKED_AT + 2 * E * C * 4 + EDGE
+QUADS0_AT = STAGED3_AT + H
 SECOND_SILU_AT = X_AT[3]
 FIRST_SILU_AT = SECOND_SILU_AT + BUFFER
 W2_AT = FIRST_SILU_AT
@@ -60,7 +61,10 @@ def tile_moe_shr_glu_silu_kernel(tc, xT, w1_words, w1_scales, w3_words, w3_scale
         w1 = keep.tile([P, E, 2 * H], U8, name="w1", align_bytes=64)
         w3 = reuse.tile([P, E, 2 * H], U8, name="w3", offset=W3_AT, align_bytes=64)
         shared_w = [keep.tile([P, 2 * H], U8, name=f"shared_w{m}", align_bytes=64) for m in range(2)]
-        shared_s = [keep.tile([P, H], U8, name=f"shared_s{m}", align_bytes=64) for m in range(2)]
+        shared_s = [
+            keep.tile([P, H], U8, name="shared_s0", align_bytes=64),
+            reuse.tile([P, H], U8, name="shared_s1", offset=QUADS0_AT, align_bytes=64),
+        ]
         planes = keep.tile([P, 2 * E * H], U8, name="planes", align_bytes=64)
         s1 = planes[:, 0 : E * H].rearrange("p (e n) -> p e n", e=E)
         s3 = planes[:, E * H : 2 * E * H].rearrange("p (e n) -> p e n", e=E)
@@ -127,8 +131,8 @@ def tile_moe_shr_glu_silu_kernel(tc, xT, w1_words, w1_scales, w3_words, w3_scale
                 words[:, 0, :].bitcast(U16).rearrange("p (c i d) -> p c d i", d=4, i=8),
             )
 
-        def permute_scales(matrix):
-            nc.vector.tensor_copy(
+        def permute_scales(matrix, copy):
+            copy(
                 shared_s[matrix][:].rearrange("p (d c i) -> p c d i", d=4, i=16),
                 staged[matrix].rearrange("p (c i d) -> p c d i", d=4, i=16),
             )
@@ -252,7 +256,7 @@ def tile_moe_shr_glu_silu_kernel(tc, xT, w1_words, w1_scales, w3_words, w3_scale
         round_pairs(0, nc.scalar.copy, 0, HALF)
         permute_words(0, w1)
         load_words(w1[:], w1_words, 0, E)
-        permute_scales(0)
+        permute_scales(0, nc.vector.tensor_copy)
         round_pairs(1, nc.vector.tensor_copy, 0, SPLIT)
         round_pairs(1, nc.scalar.copy, SPLIT, HALF)
         for r in range(4):
@@ -263,11 +267,11 @@ def tile_moe_shr_glu_silu_kernel(tc, xT, w1_words, w1_scales, w3_words, w3_scale
         load_words(w3[:], w3_words, 0, E)
 
         round_pairs(2, nc.scalar.copy, 0, UNIT)
-        flat0 = weave(pairs, 0)
+        flat0 = weave(pairs, 0, QUADS0_AT)
         round_pairs(2, nc.scalar.copy, UNIT, HALF)
         round_pairs(3, nc.vector.tensor_copy, 0, HALF)
         xq0 = quantize("x", flat0)
-        permute_scales(1)
+        permute_scales(1, nc.gpsimd.tensor_copy)
         flat1 = weave(pairs, 1)
         gather(0, UNIT, 1)
         gather(UNIT, E * C, 1)

from contextlib import ExitStack

import concourse.mybir as mybir
from concourse.masks import make_identity

F32 = mybir.dt.float32
BF16 = mybir.dt.bfloat16
I32 = mybir.dt.int32
U32 = mybir.dt.uint32
U16 = mybir.dt.uint16
U8 = mybir.dt.uint8
FP8X4 = mybir.dt.float8_e4m3fn_x4
FP4X4 = mybir.dt.float4_e2m1fn_x4
SILU = mybir.ActivationFunctionType.Silu
MULT = mybir.AluOpType.mult
ADD = mybir.AluOpType.add

P = 128
K, T, E, C, H, N = 512, 1024, 6, 128, 512, 128
SHARED = E
UNIT = 256
PARTS = UNIT // P
HALF = T // 2
SPLIT = 336
ZEROS = 256
WORK_BUFS = 7
FLOPS = 2 * (E * C + T) * (2 * K * H + H * N)

BANK = 2048
PAIRS = ((0, 1), (2, 3), (4, 5), (6, 7))
TURN_BANK, ROUTED_BANK = PAIRS[3]
RESULT_BANKS = (TURN_BANK, *PAIRS[1], PAIRS[2][0])

X_BYTES = 2 * HALF * 4
BUFFER = 2048
EDGE = 64
X_AT = (0, X_BYTES, 2 * X_BYTES, 3 * X_BYTES)
LANDED3_AT = 4 * X_BYTES
W3_AT = LANDED3_AT + 2 * H - EDGE
S2_AT = W3_AT + E * 2 * H
STAGED1_AT = S2_AT + (E + 1) * N
PICKED_AT = STAGED1_AT + H - EDGE
STAGED3_AT = PICKED_AT + 2 * E * C * 4 + EDGE
QUADS0_AT = STAGED3_AT + H
SECOND_SILU_AT = X_AT[3]
FIRST_SILU_AT = SECOND_SILU_AT + BUFFER
W2_AT = FIRST_SILU_AT
GATES_AT = SECOND_SILU_AT - BUFFER // 2


def tile_moe_shr_glu_silu_kernel(tc, xT, w1_words, w1_scales, w3_words, w3_scales, w2_words, w2_scales, gate, offs, out):
    nc = tc.nc
    with ExitStack() as ctx:
        keep = ctx.enter_context(tc.tile_pool(name="keep", bufs=1))
        reuse = ctx.enter_context(tc.tile_pool(name="reuse", bufs=1))
        work = ctx.enter_context(tc.tile_pool(name="work", bufs=WORK_BUFS))
        psum = ctx.enter_context(tc.psum_pool(name="psum", bufs=1))

        offsets = keep.tile([P, E * C // 16], U16, name="offsets")
        pairs = keep.tile([P, 2, T], U32, name="pairs", align_bytes=64)
        w1 = keep.tile([P, E, 2 * H], U8, name="w1", align_bytes=64)
        w3 = reuse.tile([P, E, 2 * H], U8, name="w3", offset=W3_AT, align_bytes=64)
        shared_w = [keep.tile([P, 2 * H], U8, name=f"shared_w{m}", align_bytes=64) for m in range(2)]
        shared_s = [
            keep.tile([P, H], U8, name="shared_s0", align_bytes=64),
            reuse.tile([P, H], U8, name="shared_s1", offset=QUADS0_AT, align_bytes=64),
        ]
        planes = keep.tile([P, 2 * E * H], U8, name="planes", align_bytes=64)
        s1 = planes[:, 0 : E * H].rearrange("p (e n) -> p e n", e=E)
        s3 = planes[:, E * H : 2 * E * H].rearrange("p (e n) -> p e n", e=E)
        border = planes[:, E * H - 2 * ZEROS : E * H + 2 * ZEROS]
        scattered = keep.tile([P, T], F32, name="scattered")
        result = keep.tile([P, T], F32, name="result")
        ident = keep.tile([P, P], F32, name="ident")

        late_zero = reuse.tile([P, (2 * X_BYTES + EDGE) // 4], F32, name="late_zero", offset=X_AT[2])
        first_zeros = reuse.tile([P, H], U8, name="first_zeros", offset=X_AT[1], align_bytes=64)
        landed3 = reuse.tile([P, 1, 2 * H], U8, name="landed3", offset=LANDED3_AT, align_bytes=64)
        staged = [
            reuse.tile([P, H], U8, name=f"staged{m}", offset=at, align_bytes=64)[:]
            for m, at in enumerate((STAGED1_AT, STAGED3_AT))
        ]
        picked = reuse.tile([P, 2, E * C], U32, name="picked", offset=PICKED_AT, align_bytes=64)
        s2 = reuse.tile([P, E + 1, N], U8, name="s2", offset=S2_AT, align_bytes=64)[:]
        raw = [reuse.tile([P, 2, HALF], F32, name=f"raw{piece}", offset=X_AT[piece], align_bytes=64) for piece in range(4)]
        w2 = reuse.tile([P, E + 1, 2 * N], U8, name="w2", offset=W2_AT, align_bytes=64)
        gates = reuse.tile([P, E * C], F32, name="gates", offset=GATES_AT, align_bytes=64)

        def load_x(piece):
            row, at = piece // 2 * 2, piece % 2 * HALF
            nc.sync.dma_start(out=raw[piece][:], in_=xT.rearrange("(p j) t -> p j t", j=4)[:, row : row + 2, at : at + HALF])

        def load_words(tile, words, a, b):
            nc.sync.dma_start(out=tile.bitcast(I32), in_=words[a:b, 0].bitcast(I32).rearrange("e p n -> p e n"))

        def load_scale_rows(plane, scales, a, b, r):
            view = scales[a:b].bitcast(I32).rearrange("e s (q r) n -> r q (e s) n", r=4)
            nc.sync.dma_start(out=plane[r:P:32].bitcast(I32), in_=view[r])

        def load_scales(plane, scales, a, b):
            for r in range(4):
                load_scale_rows(plane, scales, a, b, r)

        nc.vector.memset(first_zeros[:].bitcast(I32), 0)
        nc.vector.tensor_copy(staged[0].bitcast(I32), first_zeros[:].bitcast(I32))
        nc.vector.memset(staged[1].bitcast(I32), 0)
        nc.vector.memset(late_zero[:, 0:1], 0.0)
        nc.vector.memset(border.bitcast(I32), 0)
        nc.scalar.activation(
            scattered[:, 0:ZEROS], border.bitcast(F32), SILU, bias=staged[1][:, 0:4].bitcast(F32), scale=late_zero[:, 0:1]
        )
        nc.vector.memset(planes[:, E * H + 2 * ZEROS : 2 * E * H].bitcast(I32), 0)
        nc.vector.memset(planes[:, 0 : E * H - 2 * ZEROS].bitcast(I32), 0)
        nc.vector.memset(scattered[:, ZEROS:], 0.0)
        nc.vector.memset(s2.rearrange("p e n -> p (e n)").bitcast(I32), 0)

        nc.sync.dma_start(offsets[:], offs)
        load_words(w1[:, 0:1, :], w1_words, SHARED, SHARED + 1)
        load_x(0)
        load_scales(staged[0].rearrange("p (e n) -> p e n", e=1), w1_scales, SHARED, SHARED + 1)
        load_x(1)
        load_words(landed3[:], w3_words, SHARED, SHARED + 1)
        load_x(2)
        load_x(3)
        load_scales(staged[1].rearrange("p (e n) -> p e n", e=1), w3_scales, SHARED, SHARED + 1)
        make_identity(nc, ident[:])

        def permute_words(matrix, words):
            nc.vector.tensor_copy(
                shared_w[matrix][:].bitcast(U16).rearrange("p (d c i) -> p c d i", d=4, i=8),
                words[:, 0, :].bitcast(U16).rearrange("p (c i d) -> p c d i", d=4, i=8),
            )

        def permute_scales(matrix, copy):
            copy(
                shared_s[matrix][:].rearrange("p (d c i) -> p c d i", d=4, i=16),
                staged[matrix].rearrange("p (c i d) -> p c d i", d=4, i=16),
            )

        def scratch(shape, dtype, name, place):
            if place is None:
                return work.tile(shape, dtype, name=name, align_bytes=64)
            if isinstance(place, int):
                return reuse.tile(shape, dtype, name=f"{name}_{place}", offset=place, align_bytes=64)
            return reuse.tile(shape, dtype, name=name, tag=place, align_bytes=64)

        def round_pairs(piece, copy, a, b):
            at = piece % 2 * HALF
            copy(
                pairs[:, piece // 2, at + a : at + b].bitcast(BF16).rearrange("p (t e) -> p t e", e=2),
                raw[piece][:, :, a:b].rearrange("p e t -> p t e"),
            )

        def weave(words, unit, place=None, copy=nc.scalar.copy):
            quads = scratch([P, UNIT, 4], BF16, "quads", place)
            flat = quads[:].rearrange("p c j -> p (c j)")
            halves = words[:, :, unit * UNIT : (unit + 1) * UNIT]
            copy(flat.bitcast(U32).rearrange("p (t h) -> p t h", h=2), halves.rearrange("p h t -> p t h"))
            return flat

        def slots(a, b):
            return offsets[:, a // 16 : b // 16]

        def gather(a, b, half):
            nc.vector.tensor_copy(picked[:, half, a:b], pairs[:, half, :].indirect(slots(a, b)))

        def quantize(tag, flat):
            codes = work.tile([P, UNIT], U32, name=tag + "_codes", align_bytes=64)
            scales = work.tile([P, UNIT], U8, name=tag + "_scales", align_bytes=64)
            nc.vector.quantize_mx(out=codes[:].bitcast(FP8X4), scales=scales[:], in_=flat)
            return codes, scales

        def sum_banks(pair):
            return [psum.tile([P, 4, P], F32, name=f"sums{bank}", offset=bank * BANK) for bank in PAIRS[pair]]

        def shared_part(xq, h, part, pair, place=None, bias=0.0):
            codes, scales = xq
            cols = slice(part * P, (part + 1) * P)
            a, b = sum_banks(pair)
            for matrix, acc in enumerate((a, b)):
                for d in range(4):
                    nc.tensor.matmul_mx(
                        out=acc[:, d, :], lhsT=shared_w[matrix][:, 2 * d * P : 2 * (d + 1) * P].bitcast(FP4X4),
                        lhsT_scale=shared_s[matrix][:, d * P : (d + 1) * P],
                        rhs=codes[:, cols].bitcast(FP8X4), rhs_scale=scales[:, cols], start=True, stop=True,
                    )
            act = scratch([P, P, 4], F32, "act", place)
            nc.scalar.activation(act[:], a[:].rearrange("p d n -> p n d"), SILU, bias=bias)
            nc.vector.tensor_tensor(h[:, cols, :], act[:], b[:].rearrange("p d n -> p n d"), MULT)

        def hidden_tile():
            return work.tile([P, UNIT, 4], BF16, name="h", align_bytes=64)

        def quantize_shared(h):
            return quantize("s", h[:].rearrange("p c j -> p (c j)"))

        def routed_part(xq, e, rows, pair, place=None):
            codes, scales = xq
            cols = slice(e % PARTS * P, (e % PARTS + 1) * P)
            a, b = (acc[:].rearrange("p d n -> p (d n)") for acc in sum_banks(pair))
            for acc, w, s in ((a, w1, s1), (b, w3, s3)):
                nc.tensor.matmul_mx(
                    out=acc, lhsT=codes[:, cols].bitcast(FP8X4), lhsT_scale=scales[:, cols],
                    rhs=w[:, e, :].bitcast(FP4X4), rhs_scale=s[:, e, :], start=True, stop=True,
                )
            act = scratch([P, P, 4], F32, "act", place)
            act = act[:].rearrange("p n d -> p (n d)").rearrange("p (u m v) -> p u m v", u=2, v=2)
            nc.scalar.activation(act, a.rearrange("p (m u v) -> p u m v", u=2, v=2), SILU)
            nc.vector.tensor_tensor(
                rows[:, e % PARTS, :].rearrange("p (u m v) -> p u m v", u=2, v=2), act,
                b.rearrange("p (m u v) -> p u m v", u=2, v=2), MULT,
            )

        def turn(rows):
            back = psum.tile([P, PARTS, 2, P], F32, name="back", offset=TURN_BANK * BANK)
            for part in range(PARTS):
                words = rows[:, part, :].bitcast(F32)
                for u in range(2):
                    nc.tensor.transpose(back[:, part, u, :], words[:, u * P : (u + 1) * P], ident[:])
            flat = hidden_tile()[:].rearrange("p c j -> p (c j)")
            nc.scalar.copy(
                flat.bitcast(F32).rearrange("p (t r u) -> p t r u", t=PARTS, u=2),
                back[:].rearrange("p t u r -> p t r u"),
            )
            return flat

        def routed_result(unit, hq, place=None):
            codes, scales = hq
            y = psum.tile([P, UNIT], F32, name="y", offset=ROUTED_BANK * BANK)
            for part in range(PARTS):
                e = unit * PARTS + part
                cols = slice(part * P, (part + 1) * P)
                nc.tensor.matmul_mx(
                    out=y[:, cols], lhsT=w2[:, e, :].bitcast(FP4X4), lhsT_scale=s2[:, e, :],
                    rhs=codes[:, cols].bitcast(FP8X4), rhs_scale=scales[:, cols], start=True, stop=True,
                )
            ysb = scratch([P, UNIT], F32, "ysb", place)
            nc.scalar.copy(ysb[:], y[:])
            return ysb

        def scatter(unit, ysb):
            a, b = unit * UNIT, (unit + 1) * UNIT
            nc.vector.tensor_tensor(scattered[:].indirect(slots(a, b)), ysb[:], gates[:, a:b], MULT)

        def finish(unit, hq):
            codes, scales = hq
            cols = slice(unit * UNIT, (unit + 1) * UNIT)
            ys = psum.tile([P, UNIT], F32, name=f"ys{unit}", offset=RESULT_BANKS[unit] * BANK)
            nc.tensor.matmul_mx(
                out=ys[:], lhsT=w2[:, SHARED, :].bitcast(FP4X4), lhsT_scale=s2[:, SHARED, :],
                rhs=codes[:].bitcast(FP8X4), rhs_scale=scales[:], start=True, stop=True,
            )
            nc.vector.tensor_tensor(result[:, cols], ys[:], scattered[:, cols], ADD)
            nc.sync.dma_start(out=out[:, cols], in_=result[:, cols])

        round_pairs(0, nc.scalar.copy, 0, HALF)
        permute_words(0, w1)
        load_words(w1[:], w1_words, 0, E)
        permute_scales(0, nc.vector.tensor_copy)
        round_pairs(1, nc.vector.tensor_copy, 0, SPLIT)
        round_pairs(1, nc.scalar.copy, SPLIT, HALF)
        for r in range(4):
            load_scale_rows(s1, w1_scales, 0, E, r)
            load_scale_rows(s3, w3_scales, 0, E, r)
        gather(0, E * C, 0)
        permute_words(1, landed3)
        load_words(w3[:], w3_words, 0, E)

        round_pairs(2, nc.scalar.copy, 0, UNIT)
        flat0 = weave(pairs, 0, QUADS0_AT)
        round_pairs(2, nc.scalar.copy, UNIT, HALF)
        round_pairs(3, nc.vector.tensor_copy, 0, HALF)
        xq0 = quantize("x", flat0)
        permute_scales(1, nc.gpsimd.tensor_copy)
        flat1 = weave(pairs, 1)
        gather(0, UNIT, 1)
        gather(UNIT, E * C, 1)
        xq1 = quantize("x", flat1)
        flat_r1 = weave(picked, 1, None, nc.vector.tensor_copy)
        xq2 = quantize("x", weave(pairs, 2))
        r1 = quantize("x", flat_r1)

        h0, h1, h2, h3 = (hidden_tile() for unit in range(4))
        shared_part(xq0, h0, 0, 0, FIRST_SILU_AT, s2[:, 0, 0:4].bitcast(F32))
        load_scales(s2, w2_scales, 0, E + 1)
        load_words(w2[:], w2_words, 0, E + 1)
        r0 = quantize("x", weave(picked, 0))
        shared_part(xq0, h0, 1, 1, SECOND_SILU_AT)
        nc.sync.dma_start(out=gates[:], in_=gate)
        shared_part(xq1, h1, 0, 2)
        sq0 = quantize_shared(h0)
        shared_part(xq1, h1, 1, 3)
        shared_part(xq2, h2, 0, 0)
        r2 = quantize("x", weave(picked, 2))
        shared_part(xq2, h2, 1, 1)
        sq1 = quantize_shared(h1)

        rows0, rows1, rows2 = (work.tile([P, PARTS, H], BF16, name="rows", align_bytes=64) for unit in range(3))
        routed_part(r0, 0, rows0, 2)
        routed_part(r0, 1, rows0, 0)
        sq2 = quantize_shared(h2)
        routed_part(r1, 2, rows1, 1)
        routed_part(r1, 3, rows1, 2, "before_last_unit")
        hq0 = quantize("h", turn(rows0))
        routed_part(r2, 4, rows2, 0)
        routed_part(r2, 5, rows2, 1, "before_scatter0")
        hq1 = quantize("h", turn(rows1))
        y0 = routed_result(0, hq0, "before_scatter0")
        xq3 = quantize("x", weave(pairs, 3, "before_last_unit"))
        scatter(0, y0)
        shared_part(xq3, h3, 0, 2, "before_scatter1")
        hq2 = quantize("h", turn(rows2))
        y1 = routed_result(1, hq1, "before_scatter1")
        shared_part(xq3, h3, 1, 0)
        scatter(1, y1)
        scatter(2, routed_result(2, hq2))
        sq3 = quantize_shared(h3)

        for unit, sq in enumerate((sq0, sq1, sq2, sq3)):
            finish(unit, sq)
